import numpy as np
import ml_dtypes


def mxq(x, axis, fmt="e4m3"):
    dtype, down = {"e4m3": (ml_dtypes.float8_e4m3fn, 7), "e5m2": (ml_dtypes.float8_e5m2, 14)}[fmt]
    v = np.moveaxis(np.asarray(x, np.float32).astype(ml_dtypes.bfloat16).astype(np.float64), axis, -1)
    blocks = v.reshape(v.shape[:-1] + (-1, 32))
    amax = np.abs(blocks).max(-1, keepdims=True)
    byte = np.maximum(np.where(amax > 0, np.frexp(amax)[1] - 1 + 127, 0) - down, 1)
    scale = np.exp2(byte - 127.0)
    codes = (blocks / scale).astype(np.float32).astype(dtype).astype(np.float64)
    return np.moveaxis((codes * scale).reshape(v.shape), -1, axis)


WIDE = False


def mx_kscale(k):
    if not WIDE:
        return np.ones(k)
    levels = np.array([10, -10, 5, -5, 0])
    if k % 512:
        return np.exp2(np.random.permutation(np.resize(levels, k // 32))).repeat(32)
    a = np.empty((k // 512, 16))
    for p in range(k // 512):
        a[p, :8] = np.random.permutation(np.resize(levels, 8))
        for g in range(8):
            far = levels[np.abs(levels - a[p, g]) >= 10]
            a[p, g + 8] = far[np.random.randint(len(far))]
    return np.exp2(a.ravel()).repeat(32)


def f64(x):
    return np.asarray(x).astype(np.float64)


def striped(idx):
    return np.tile(idx.reshape(-1, 16).T, (8, 1)).astype(np.uint16)


def unstriped(offs):
    return offs[:16].T.reshape(-1).astype(np.int64)


def gelu(v):
    return 0.5 * v * (1.0 + np.tanh(np.sqrt(2.0 / np.pi) * (v + 0.044715 * v**3)))


K, T, E, C, N = 2048, 1024, 16, 128, 128


def by_expert(wq, xq):
    return np.concatenate([wq[e].T @ xq[:, e * C:(e + 1) * C] for e in range(E)], axis=1)


def setup_inputs():
    n = np.random.standard_normal
    s = mx_kscale(K)[:, None]
    first = np.random.permutation(np.repeat(np.arange(E), T // E))
    second = (first + 1 + np.random.permutation(np.repeat(np.arange(E - 1), -(-T // (E - 1)))[:T])) % E
    while np.bincount(second, minlength=E).max() != T // E:
        load = np.bincount(second, minlength=E); hi, lo = int(load.argmax()), int(load.argmin())
        t = np.flatnonzero((second == hi) & (first != lo))[0]; second[t] = lo
    slot_token = np.empty(E * C, np.int64); pos = np.empty((2, T), np.int64); fill = np.zeros(E, np.int64)
    place = np.stack([np.random.permutation(C) for _ in range(E)])
    for r, deal in enumerate((first, second)):
        for t in np.random.permutation(T):
            e = deal[t]; j = e * C + place[e, fill[e]]; fill[e] += 1; slot_token[j] = t; pos[r, t] = j
    g = np.random.uniform(0.2, 0.8, T)
    return {
        "xT": (n((K, T)) * s).astype(np.float32),
        "w": (n((E, K, N)) / np.sqrt(K) / s[None]).astype(np.float32),
        "b": (0.3 * n((N, E))).astype(np.float32),
        "gate": np.stack([np.tile(g, (N, 1)), np.tile(1.0 - g, (N, 1))]).astype(np.float32),
        "offs": striped(slot_token),
        "pos1": striped(pos[0]),
        "pos2": striped(pos[1]),
    }


def reference(xT, w, b, gate, offs, pos1, pos2):
    idx = unstriped(offs)
    xq = mxq(f64(xT)[:, idx], 0, "e4m3")
    y = by_expert(mxq(f64(w), 1, "e4m3"), xq)
    y = gelu(y + np.repeat(f64(b), C, axis=1))
    return f64(gate[0]) * y[:, unstriped(pos1)] + f64(gate[1]) * y[:, unstriped(pos2)]

@@ -1,0 +1,187 @@
+from contextlib import ExitStack
+
+import concourse.mybir as mybir
+
+K, T, E, C, N = 2048, 1024, 16, 128, 128
+FLOPS = 2 * K * E * C * N
+
+F32 = mybir.dt.float32
+BF16 = mybir.dt.bfloat16
+U32 = mybir.dt.uint32
+U16 = mybir.dt.uint16
+U8 = mybir.dt.uint8
+FP8X4 = mybir.dt.float8_e4m3fn_x4
+MULT, ADD = mybir.AluOpType.mult, mybir.AluOpType.add
+GELU = mybir.ActivationFunctionType.Gelu_apprx_tanh
+
+P = 128
+PASSES = K // 512
+HALF = T // 2
+SLOTS = E * C
+GROUP = 512
+EARLY = 512
+EARLY_PASSES = 2
+
+X_ON_VECTOR = (0, 1)
+W_ON_VECTOR = (7, 10, 11, 13)
+BIAS_GROUP = 4
+BIAS_LAG = 5
+PIECES = (448, 416, 160)
+BYTES_PASS = PASSES
+DELAY = 5
+PER_GROUP = GROUP // C
+AHEAD = 3
+
+
+def tile_routed_moe_kernel(tc, xT, w, b, gate, offs, pos1, pos2, out):
+    nc = tc.nc
+    with ExitStack() as ctx:
+        keep = ctx.enter_context(tc.tile_pool(name="keep", bufs=1))
+        raws = ctx.enter_context(tc.tile_pool(name="raws", bufs=10))
+        stage = ctx.enter_context(tc.tile_pool(name="stage", bufs=8))
+        wts = ctx.enter_context(tc.tile_pool(name="wts", bufs=12))
+        slots_pool = ctx.enter_context(tc.tile_pool(name="slots_pool", bufs=AHEAD))
+        work = ctx.enter_context(tc.tile_pool(name="work", bufs=3))
+        psum = ctx.enter_context(tc.psum_pool(name="psum", bufs=8))
+
+        dummy = keep.tile([P, 2], F32, name="dummy")
+        nc.gpsimd.memset(dummy[:], 0.0)
+        nc.scalar.activation(dummy[:, 1:2], dummy[:, 0:1], GELU)
+        x_scales = keep.tile([P, T], U8, name="x_scales", align_bytes=64)
+        nc.gpsimd.memset(x_scales[:], 0)
+
+        offs_sb = keep.tile([P, SLOTS // 16], U16, name="offs_sb")
+        pos1_sb = keep.tile([P, T // 16], U16, name="pos1_sb")
+        pos2_sb = keep.tile([P, T // 16], U16, name="pos2_sb")
+        y = keep.tile([P, SLOTS], F32, name="y")
+        gates = keep.tile([P, 2, T], F32, name="gates")
+        x_words = []
+        for a in range(PASSES):
+            xw = keep.tile([P, T], U32, name=f"x_words{a}", align_bytes=64)
+            x_words.append(xw)
+
+        groups = {}
+        early_words = []
+        for a in range(EARLY_PASSES):
+            ew = keep.tile([P, SLOTS], U32, name=f"early_words{a}", align_bytes=64)
+            early_words.append(ew)
+
+        def gather_early(a):
+            for s in range(0, SLOTS, EARLY):
+                idx = offs_sb[:, s // 16 : (s + EARLY) // 16]
+                nc.vector.tensor_copy(early_words[a][:, s : s + EARLY], x_words[a][:].indirect(idx))
+
+        def gather_late(g):
+            idx = offs_sb[:, g * GROUP // 16 : (g + 1) * GROUP // 16]
+            for a in range(EARLY_PASSES, PASSES):
+                got = slots_pool.tile([P, GROUP], U32, name=f"slot_words{a}", align_bytes=64)
+                nc.vector.tensor_copy(got[:], x_words[a][:].indirect(idx))
+                groups[a, g] = got
+            got = slots_pool.tile([P, GROUP], U8, name="slot_scales", align_bytes=64)
+            nc.vector.tensor_copy(got[:], x_scales[:].indirect(idx))
+            groups[BYTES_PASS, g] = got
+
+        weights = {}
+        biases = {}
+
+        def load_biases(after):
+            for e0 in range(0, E, BIAS_GROUP):
+                if min(e0 + BIAS_LAG, E - 1) == after:
+                    bias = keep.tile([P, BIAS_GROUP], F32, name=f"bias{e0}")
+                    nc.sync.dma_start(bias[:], b[:, e0 : e0 + BIAS_GROUP])
+                    for e in range(e0, e0 + BIAS_GROUP):
+                        biases[e] = bias[:, e - e0 : e - e0 + 1]
+
+        def multiply(e):
+            w_words, w_scales = weights[e]
+            sums = psum.tile([P, C], F32, name="sums")
+            slots = slice(e * C, (e + 1) * C)
+            g = e // PER_GROUP
+            part = slice(e % PER_GROUP * C, (e % PER_GROUP + 1) * C)
+            for a in range(PASSES):
+                words = early_words[a][:, slots] if a < EARLY_PASSES else groups[a, g][:, part]
+                nc.tensor.matmul_mx(
+                    out=sums[:],
+                    lhsT=w_words[:, a].bitcast(FP8X4),
+                    lhsT_scale=w_scales[:, a],
+                    rhs=words.bitcast(FP8X4),
+                    rhs_scale=groups[BYTES_PASS, g][4 * a : P, part],
+                    start=(a == 0),
+                    stop=(a == PASSES - 1),
+                )
+            nc.scalar.activation(y[:, slots], sums[:], GELU, bias=biases[e])
+            if (e + 1) % PER_GROUP == 0 and g + AHEAD < SLOTS // GROUP:
+                gather_late(g + AHEAD)
+
+        for i in range(2 * PASSES):
+            a, h = divmod(i, 2)
+            cols = slice(h * HALF, (h + 1) * HALF)
+            raw = raws.tile([P, 4, HALF], F32, name="raw")
+            nc.sync.dma_start(
+                out=raw[:],
+                in_=xT[a * 512 : (a + 1) * 512, cols].rearrange("(p j) t -> p j t", j=4),
+            )
+            if i == 0:
+                nc.sync.dma_start(offs_sb[:], offs)
+            grouped = stage.tile([P, HALF, 4], BF16, name="grouped", align_bytes=64)
+            src = raw[:].rearrange("p j (c i) -> p c j i", i=4)
+            dst = grouped[:].rearrange("p (c i) j -> p c j i", i=4)
+            if i in X_ON_VECTOR:
+                nc.vector.tensor_copy(dst, src)
+            else:
+                nc.scalar.copy(dst, src)
+            nc.vector.quantize_mx(
+                out=x_words[a][:, cols].bitcast(FP8X4),
+                scales=x_scales[4 * a : P, cols],
+                in_=grouped[:].rearrange("p t j -> p (t j)"),
+            )
+            if h == 1 and a < EARLY_PASSES:
+                gather_early(a)
+        for g in range(AHEAD):
+            gather_late(g)
+
+        for e in range(E):
+            cuts = ((0, 2, True), (2, 3, False), (3, 4, False)) if e == E - 1 else ((0, PASSES, e in W_ON_VECTOR),)
+            w_words = wts.tile([P, PASSES, N], U32, name="w_words", align_bytes=64)
+            w_scales = wts.tile([P, PASSES, N], U8, name="w_scales", align_bytes=64)
+            rows = w[e].rearrange("(a p j) n -> p a j n", p=P, j=4)
+            for a0, a1, on_vector in cuts:
+                raw = raws.tile([P, a1 - a0, 4, N], F32, name="raw")
+                nc.sync.dma_start(out=raw[:], in_=rows[:, a0:a1])
+                grouped = stage.tile([P, a1 - a0, N, 4], BF16, name="grouped", align_bytes=64)
+                src = raw[:].rearrange("p a j (c i) -> p a c j i", i=4)
+                dst = grouped[:].rearrange("p a (c i) j -> p a c j i", i=4)
+                if on_vector:
+                    nc.vector.tensor_copy(dst, src)
+                else:
+                    nc.scalar.copy(dst, src)
+                nc.vector.quantize_mx(
+                    out=w_words[:, a0:a1].rearrange("p a n -> p (a n)").bitcast(FP8X4),
+                    scales=w_scales[:, a0:a1].rearrange("p a n -> p (a n)"),
+                    in_=grouped[:].rearrange("p a n j -> p (a n j)"),
+                )
+            if e == 1:
+                nc.sync.dma_start(pos1_sb[:], pos1)
+                nc.sync.dma_start(pos2_sb[:], pos2)
+            weights[e] = (w_words, w_scales)
+            load_biases(e)
+            if e >= DELAY:
+                multiply(e - DELAY)
+        nc.sync.dma_start(gates[:, 0], gate[0])
+        for cols in (slice(0, PIECES[0]), slice(PIECES[0], T)):
+            nc.sync.dma_start(gates[:, 1, cols], gate[1, :, cols])
+        for e in range(E - DELAY, E):
+            multiply(e)
+
+        first = keep.tile([P, T], F32, name="first")
+        nc.vector.tensor_tensor(first[:], y[:].indirect(pos1_sb[:]), gates[:, 0], MULT)
+        t = 0
+        for width in PIECES:
+            cols = slice(t, t + width)
+            idx = slice(t // 16, (t + width) // 16)
+            second = work.tile([P, width], F32, name="second")
+            total = work.tile([P, width], F32, name="total")
+            nc.vector.tensor_tensor(second[:], y[:].indirect(pos2_sb[:, idx]), gates[:, 1, cols], MULT)
+            nc.vector.tensor_tensor(total[:], first[:, cols], second[:], ADD)
+            nc.sync.dma_start(out=out[:, cols], in_=total[:])
+            t += width

@@ -18,30 +18,24 @@ P = 128
 PASSES = K // 512
 HALF = T // 2
 SLOTS = E * C
-GROUP = 512
-EARLY = 512
-EARLY_PASSES = 2
-
-X_ON_VECTOR = (0, 1)
-W_ON_VECTOR = (7, 10, 11, 13)
-BIAS_GROUP = 4
-BIAS_LAG = 5
-PIECES = (448, 416, 160)
-BYTES_PASS = PASSES
-DELAY = 5
-PER_GROUP = GROUP // C
-AHEAD = 3
+GATHERS = (768, 768, 512)
+PAIRED = 12
+SHARED_FROM = 6
+HALVED = 2
+BANKED = 8
+BIASES_BEHIND = (10,)
+PIECES = (576, 320, 128)
 
 
 def tile_routed_moe_kernel(tc, xT, w, b, gate, offs, pos1, pos2, out):
     nc = tc.nc
     with ExitStack() as ctx:
         keep = ctx.enter_context(tc.tile_pool(name="keep", bufs=1))
-        raws = ctx.enter_context(tc.tile_pool(name="raws", bufs=10))
+        big = ctx.enter_context(tc.tile_pool(name="big", bufs=4))
+        small = ctx.enter_context(tc.tile_pool(name="small", bufs=3))
         stage = ctx.enter_context(tc.tile_pool(name="stage", bufs=8))
-        wts = ctx.enter_context(tc.tile_pool(name="wts", bufs=12))
-        slots_pool = ctx.enter_context(tc.tile_pool(name="slots_pool", bufs=AHEAD))
-        work = ctx.enter_context(tc.tile_pool(name="work", bufs=3))
+        wts = ctx.enter_context(tc.tile_pool(name="wts", bufs=6))
+        work = ctx.enter_context(tc.tile_pool(name="work", bufs=len(PIECES)))
         psum = ctx.enter_context(tc.psum_pool(name="psum", bufs=8))
 
         dummy = keep.tile([P, 2], F32, name="dummy")
@@ -55,133 +49,158 @@ def tile_routed_moe_kernel(tc, xT, w, b, gate, offs, pos1, pos2, out):
         pos2_sb = keep.tile([P, T // 16], U16, name="pos2_sb")
         y = keep.tile([P, SLOTS], F32, name="y")
         gates = keep.tile([P, 2, T], F32, name="gates")
-        x_words = []
+        slot_scales = keep.tile([P, SLOTS], U8, name="slot_scales", align_bytes=64)
+        x_words, slot_words = [], []
         for a in range(PASSES):
-            xw = keep.tile([P, T], U32, name=f"x_words{a}", align_bytes=64)
-            x_words.append(xw)
+            x_words.append(keep.tile([P, T], U32, name=f"x_words{a}", align_bytes=64))
+            slot_words.append(keep.tile([P, SLOTS], U32, name=f"slot_words{a}", align_bytes=64))
 
-        groups = {}
-        early_words = []
-        for a in range(EARLY_PASSES):
-            ew = keep.tile([P, SLOTS], U32, name=f"early_words{a}", align_bytes=64)
-            early_words.append(ew)
+        def gather(dst, window):
+            s = 0
+            for width in GATHERS:
+                idx = offs_sb[:, s // 16 : (s + width) // 16]
+                nc.vector.tensor_copy(dst[:, s : s + width], window[:].indirect(idx))
+                s += width
 
-        def gather_early(a):
-            for s in range(0, SLOTS, EARLY):
-                idx = offs_sb[:, s // 16 : (s + EARLY) // 16]
-                nc.vector.tensor_copy(early_words[a][:, s : s + EARLY], x_words[a][:].indirect(idx))
-
-        def gather_late(g):
-            idx = offs_sb[:, g * GROUP // 16 : (g + 1) * GROUP // 16]
-            for a in range(EARLY_PASSES, PASSES):
-                got = slots_pool.tile([P, GROUP], U32, name=f"slot_words{a}", align_bytes=64)
-                nc.vector.tensor_copy(got[:], x_words[a][:].indirect(idx))
-                groups[a, g] = got
-            got = slots_pool.tile([P, GROUP], U8, name="slot_scales", align_bytes=64)
-            nc.vector.tensor_copy(got[:], x_scales[:].indirect(idx))
-            groups[BYTES_PASS, g] = got
-
-        weights = {}
-        biases = {}
-
-        def load_biases(after):
-            for e0 in range(0, E, BIAS_GROUP):
-                if min(e0 + BIAS_LAG, E - 1) == after:
-                    bias = keep.tile([P, BIAS_GROUP], F32, name=f"bias{e0}")
-                    nc.sync.dma_start(bias[:], b[:, e0 : e0 + BIAS_GROUP])
-                    for e in range(e0, e0 + BIAS_GROUP):
-                        biases[e] = bias[:, e - e0 : e - e0 + 1]
-
-        def multiply(e):
-            w_words, w_scales = weights[e]
-            sums = psum.tile([P, C], F32, name="sums")
-            slots = slice(e * C, (e + 1) * C)
-            g = e // PER_GROUP
-            part = slice(e % PER_GROUP * C, (e % PER_GROUP + 1) * C)
-            for a in range(PASSES):
-                words = early_words[a][:, slots] if a < EARLY_PASSES else groups[a, g][:, part]
-                nc.tensor.matmul_mx(
-                    out=sums[:],
-                    lhsT=w_words[:, a].bitcast(FP8X4),
-                    lhsT_scale=w_scales[:, a],
-                    rhs=words.bitcast(FP8X4),
-                    rhs_scale=groups[BYTES_PASS, g][4 * a : P, part],
-                    start=(a == 0),
-                    stop=(a == PASSES - 1),
-                )
-            nc.scalar.activation(y[:, slots], sums[:], GELU, bias=biases[e])
-            if (e + 1) % PER_GROUP == 0 and g + AHEAD < SLOTS // GROUP:
-                gather_late(g + AHEAD)
-
-        for i in range(2 * PASSES):
-            a, h = divmod(i, 2)
-            cols = slice(h * HALF, (h + 1) * HALF)
-            raw = raws.tile([P, 4, HALF], F32, name="raw")
-            nc.sync.dma_start(
-                out=raw[:],
-                in_=xT[a * 512 : (a + 1) * 512, cols].rearrange("(p j) t -> p j t", j=4),
-            )
-            if i == 0:
-                nc.sync.dma_start(offs_sb[:], offs)
-            grouped = stage.tile([P, HALF, 4], BF16, name="grouped", align_bytes=64)
-            src = raw[:].rearrange("p j (c i) -> p c j i", i=4)
-            dst = grouped[:].rearrange("p (c i) j -> p c j i", i=4)
-            if i in X_ON_VECTOR:
+        def interleave(on_vector, dst, src):
+            if on_vector:
                 nc.vector.tensor_copy(dst, src)
             else:
                 nc.scalar.copy(dst, src)
+
+        def quantise_tokens(a, h, raw, on_vector):
+            cols = slice(h * HALF, (h + 1) * HALF)
+            grouped = stage.tile([P, HALF, 4], BF16, name="grouped", align_bytes=64)
+            interleave(
+                on_vector,
+                grouped[:].rearrange("p (c i) j -> p c j i", i=4),
+                raw.rearrange("p j (c i) -> p c j i", i=4),
+            )
             nc.vector.quantize_mx(
                 out=x_words[a][:, cols].bitcast(FP8X4),
                 scales=x_scales[4 * a : P, cols],
                 in_=grouped[:].rearrange("p t j -> p (t j)"),
             )
-            if h == 1 and a < EARLY_PASSES:
-                gather_early(a)
-        for g in range(AHEAD):
-            gather_late(g)
 
-        for e in range(E):
-            cuts = ((0, 2, True), (2, 3, False), (3, 4, False)) if e == E - 1 else ((0, PASSES, e in W_ON_VECTOR),)
-            w_words = wts.tile([P, PASSES, N], U32, name="w_words", align_bytes=64)
-            w_scales = wts.tile([P, PASSES, N], U8, name="w_scales", align_bytes=64)
-            rows = w[e].rearrange("(a p j) n -> p a j n", p=P, j=4)
-            for a0, a1, on_vector in cuts:
-                raw = raws.tile([P, a1 - a0, 4, N], F32, name="raw")
-                nc.sync.dma_start(out=raw[:], in_=rows[:, a0:a1])
-                grouped = stage.tile([P, a1 - a0, N, 4], BF16, name="grouped", align_bytes=64)
-                src = raw[:].rearrange("p a j (c i) -> p a c j i", i=4)
-                dst = grouped[:].rearrange("p a (c i) j -> p a c j i", i=4)
-                if on_vector:
-                    nc.vector.tensor_copy(dst, src)
-                else:
-                    nc.scalar.copy(dst, src)
-                nc.vector.quantize_mx(
-                    out=w_words[:, a0:a1].rearrange("p a n -> p (a n)").bitcast(FP8X4),
-                    scales=w_scales[:, a0:a1].rearrange("p a n -> p (a n)"),
-                    in_=grouped[:].rearrange("p a n j -> p (a n j)"),
+        weights = {}
+
+        def quantise_weights(e, a0, a1, raw, on_vector):
+            if e not in weights:
+                w_words = wts.tile([P, PASSES, N], U32, name="w_words", align_bytes=64)
+                w_scales = wts.tile([P, PASSES, N], U8, name="w_scales", align_bytes=64)
+                weights[e] = (w_words, w_scales)
+            w_words, w_scales = weights[e]
+            grouped = stage.tile([P, a1 - a0, N, 4], BF16, name="grouped", align_bytes=64)
+            interleave(
+                on_vector,
+                grouped[:].rearrange("p a (c i) j -> p a c j i", i=4),
+                raw.rearrange("p a j (c i) -> p a c j i", i=4),
+            )
+            nc.vector.quantize_mx(
+                out=w_words[:, a0:a1].rearrange("p a n -> p (a n)").bitcast(FP8X4),
+                scales=w_scales[:, a0:a1].rearrange("p a n -> p (a n)"),
+                in_=grouped[:].rearrange("p a n j -> p (a n j)"),
+            )
+
+        sums = {}
+
+        def multiply(e):
+            w_words, w_scales = weights[e]
+            if e >= BANKED:
+                sums[e] = psum.tile([P, C], F32, name="sums")
+            elif e % 4 == 0:
+                bank = psum.tile([P, 4, C], F32, name="sums")
+                for i in range(4):
+                    sums[e + i] = bank[:, i]
+            slots = slice(e * C, (e + 1) * C)
+            for a in range(PASSES):
+                nc.tensor.matmul_mx(
+                    out=sums[e][:],
+                    lhsT=w_words[:, a].bitcast(FP8X4),
+                    lhsT_scale=w_scales[:, a],
+                    rhs=slot_words[a][:, slots].bitcast(FP8X4),
+                    rhs_scale=slot_scales[4 * a : P, slots],
+                    start=(a == 0),
+                    stop=(a == PASSES - 1),
                 )
-            if e == 1:
-                nc.sync.dma_start(pos1_sb[:], pos1)
-                nc.sync.dma_start(pos2_sb[:], pos2)
-            weights[e] = (w_words, w_scales)
-            load_biases(e)
-            if e >= DELAY:
-                multiply(e - DELAY)
+
+        def load_biases(e0, e1):
+            biases = keep.tile([P, e1 - e0], F32, name=f"biases{e0}")
+            nc.sync.dma_start(biases[:], b[:, e0:e1])
+            return biases
+
+        def activate(e0, e1, biases):
+            for e in range(e0, e1):
+                nc.scalar.activation(y[:, e * C : (e + 1) * C], sums[e][:], GELU, bias=biases[:, e - e0 : e - e0 + 1])
+
+        x_rows = xT.rearrange("(a p j) t -> a p j t", p=P, j=4)
+        for a in range(PASSES):
+            if a >= HALVED:
+                raw = big.tile([P, 4, T], F32, name="raw_big")
+                nc.sync.dma_start(out=raw[:], in_=x_rows[a])
+            for h in range(2):
+                cols = slice(h * HALF, (h + 1) * HALF)
+                if a < HALVED:
+                    half = small.tile([P, 4, HALF], F32, name="raw_small")
+                    nc.sync.dma_start(out=half[:], in_=x_rows[a, :, :, cols])
+                    quantise_tokens(a, h, half[:], a == 0)
+                else:
+                    quantise_tokens(a, h, raw[:, :, cols], False)
+            if a == 0:
+                nc.sync.dma_start(offs_sb[:], offs)
+            gather(slot_words[a], x_words[a])
+        gather(slot_scales, x_scales)
+
+        w_rows = w.rearrange("e (a p j) n -> p e a j n", p=P, j=4)
+        done = 0
+        for e0 in list(range(0, PAIRED, 2)) + list(range(PAIRED, E - 1)):
+            if e0 < PAIRED:
+                raw = big.tile([P, 2, PASSES, 4, N], F32, name="raw_big")
+                nc.sync.dma_start(out=raw[:], in_=w_rows[:, e0 : e0 + 2])
+                if e0 >= SHARED_FROM:
+                    units = ((e0 + 1, 0, PASSES, raw[:, 1], True), (e0, 0, PASSES, raw[:, 0], False))
+                else:
+                    units = ((e0, 0, PASSES, raw[:, 0], False), (e0 + 1, 0, PASSES, raw[:, 1], False))
+            else:
+                raw = small.tile([P, PASSES, 4, N], F32, name="raw_small")
+                nc.sync.dma_start(out=raw[:], in_=w_rows[:, e0])
+                units = ((e0, 0, 2, raw[:, 0:2], True), (e0, 2, 4, raw[:, 2:4], False))
+            if e0 in BIASES_BEHIND:
+                biases = load_biases(done, e0)
+            for unit in units:
+                quantise_weights(*unit)
+            if e0 in BIASES_BEHIND:
+                activate(done, e0, biases)
+                done = e0
+            for e in sorted(set(unit[0] for unit in units)):
+                multiply(e)
+        for a0, a1, on_vector in ((0, 2, False), (2, 3, True), (3, 4, False)):
+            raw = keep.tile([P, a1 - a0, 4, N], F32, name=f"raw_last{a0}")
+            nc.sync.dma_start(out=raw[:], in_=w_rows[:, E - 1, a0:a1])
+            quantise_weights(E - 1, a0, a1, raw[:], on_vector)
+        biases = load_biases(done, E)
+        nc.sync.dma_start(pos1_sb[:], pos1)
         nc.sync.dma_start(gates[:, 0], gate[0])
-        for cols in (slice(0, PIECES[0]), slice(PIECES[0], T)):
-            nc.sync.dma_start(gates[:, 1, cols], gate[1, :, cols])
-        for e in range(E - DELAY, E):
-            multiply(e)
+        nc.sync.dma_start(pos2_sb[:], pos2)
+        nc.sync.dma_start(gates[:, 1], gate[1])
+        activate(done, E - 1, biases)
+        multiply(E - 1)
+        activate(E - 1, E, biases[:, E - 1 - done : E - done])
 
         first = keep.tile([P, T], F32, name="first")
         nc.vector.tensor_tensor(first[:], y[:].indirect(pos1_sb[:]), gates[:, 0], MULT)
-        t = 0
-        for width in PIECES:
-            cols = slice(t, t + width)
-            idx = slice(t // 16, (t + width) // 16)
-            second = work.tile([P, width], F32, name="second")
-            total = work.tile([P, width], F32, name="total")
-            nc.vector.tensor_tensor(second[:], y[:].indirect(pos2_sb[:, idx]), gates[:, 1, cols], MULT)
-            nc.vector.tensor_tensor(total[:], first[:, cols], second[:], ADD)
-            nc.sync.dma_start(out=out[:, cols], in_=total[:])
-            t += width
+        starts = [sum(PIECES[:i]) for i in range(len(PIECES) + 1)]
+        seconds = []
+        for i in range(len(PIECES) + 1):
+            if i < len(PIECES):
+                idx = slice(starts[i] // 16, starts[i + 1] // 16)
+                second = work.tile([P, PIECES[i]], F32, name="second")
+                nc.vector.tensor_tensor(
+                    second[:], y[:].indirect(pos2_sb[:, idx]), gates[:, 1, starts[i] : starts[i + 1]], MULT
+                )
+                seconds.append(second)
+            if i > 0:
+                cols = slice(starts[i - 1], starts[i])
+                total = work.tile([P, PIECES[i - 1]], F32, name="total")
+                nc.vector.tensor_tensor(total[:], first[:, cols], seconds[i - 1][:], ADD)
+                nc.sync.dma_start(out=out[:, cols], in_=total[:])

@@ -15,6 +15,7 @@ MULT, ADD = mybir.AluOpType.mult, mybir.AluOpType.add
 GELU = mybir.ActivationFunctionType.Gelu_apprx_tanh
 
 P = 128
+ALIGN = 256
 PASSES = K // 512
 HALF = T // 2
 SLOTS = E * C
@@ -41,19 +42,19 @@ def tile_routed_moe_kernel(tc, xT, w, b, gate, offs, pos1, pos2, out):
         dummy = keep.tile([P, 2], F32, name="dummy")
         nc.gpsimd.memset(dummy[:], 0.0)
         nc.scalar.activation(dummy[:, 1:2], dummy[:, 0:1], GELU)
-        x_scales = keep.tile([P, T], U8, name="x_scales", align_bytes=64)
+        x_scales = keep.tile([P, T], U8, name="x_scales", align_bytes=ALIGN)
         nc.gpsimd.memset(x_scales[:], 0)
 
         offs_sb = keep.tile([P, SLOTS // 16], U16, name="offs_sb")
         pos1_sb = keep.tile([P, T // 16], U16, name="pos1_sb")
         pos2_sb = keep.tile([P, T // 16], U16, name="pos2_sb")
-        y = keep.tile([P, SLOTS], F32, name="y")
-        gates = keep.tile([P, 2, T], F32, name="gates")
-        slot_scales = keep.tile([P, SLOTS], U8, name="slot_scales", align_bytes=64)
+        y = keep.tile([P, SLOTS], F32, name="y", align_bytes=ALIGN)
+        gates = keep.tile([P, 2, T], F32, name="gates", align_bytes=ALIGN)
+        slot_scales = keep.tile([P, SLOTS], U8, name="slot_scales", align_bytes=ALIGN)
         x_words, slot_words = [], []
         for a in range(PASSES):
-            x_words.append(keep.tile([P, T], U32, name=f"x_words{a}", align_bytes=64))
-            slot_words.append(keep.tile([P, SLOTS], U32, name=f"slot_words{a}", align_bytes=64))
+            x_words.append(keep.tile([P, T], U32, name=f"x_words{a}", align_bytes=ALIGN))
+            slot_words.append(keep.tile([P, SLOTS], U32, name=f"slot_words{a}", align_bytes=ALIGN))
 
         def gather(dst, window):
             s = 0
@@ -70,7 +71,7 @@ def tile_routed_moe_kernel(tc, xT, w, b, gate, offs, pos1, pos2, out):
 
         def quantise_tokens(a, h, raw, on_vector):
             cols = slice(h * HALF, (h + 1) * HALF)
-            grouped = stage.tile([P, HALF, 4], BF16, name="grouped", align_bytes=64)
+            grouped = stage.tile([P, HALF, 4], BF16, name="grouped", align_bytes=ALIGN)
             interleave(
                 on_vector,
                 grouped[:].rearrange("p (c i) j -> p c j i", i=4),
@@ -86,11 +87,11 @@ def tile_routed_moe_kernel(tc, xT, w, b, gate, offs, pos1, pos2, out):
 
         def quantise_weights(e, a0, a1, raw, on_vector):
             if e not in weights:
-                w_words = wts.tile([P, PASSES, N], U32, name="w_words", align_bytes=64)
-                w_scales = wts.tile([P, PASSES, N], U8, name="w_scales", align_bytes=64)
+                w_words = wts.tile([P, PASSES, N], U32, name="w_words", align_bytes=ALIGN)
+                w_scales = wts.tile([P, PASSES, N], U8, name="w_scales", align_bytes=ALIGN)
                 weights[e] = (w_words, w_scales)
             w_words, w_scales = weights[e]
-            grouped = stage.tile([P, a1 - a0, N, 4], BF16, name="grouped", align_bytes=64)
+            grouped = stage.tile([P, a1 - a0, N, 4], BF16, name="grouped", align_bytes=ALIGN)
             interleave(
                 on_vector,
                 grouped[:].rearrange("p a (c i) j -> p a c j i", i=4),
@@ -136,12 +137,12 @@ def tile_routed_moe_kernel(tc, xT, w, b, gate, offs, pos1, pos2, out):
         x_rows = xT.rearrange("(a p j) t -> a p j t", p=P, j=4)
         for a in range(PASSES):
             if a >= HALVED:
-                raw = big.tile([P, 4, T], F32, name="raw_big")
+                raw = big.tile([P, 4, T], F32, name="raw_big", align_bytes=ALIGN)
                 nc.sync.dma_start(out=raw[:], in_=x_rows[a])
             for h in range(2):
                 cols = slice(h * HALF, (h + 1) * HALF)
                 if a < HALVED:
-                    half = small.tile([P, 4, HALF], F32, name="raw_small")
+                    half = small.tile([P, 4, HALF], F32, name="raw_small", align_bytes=ALIGN)
                     nc.sync.dma_start(out=half[:], in_=x_rows[a, :, :, cols])
                     quantise_tokens(a, h, half[:], a == 0)
                 else:
@@ -155,14 +156,14 @@ def tile_routed_moe_kernel(tc, xT, w, b, gate, offs, pos1, pos2, out):
         done = 0
         for e0 in list(range(0, PAIRED, 2)) + list(range(PAIRED, E - 1)):
             if e0 < PAIRED:
-                raw = big.tile([P, 2, PASSES, 4, N], F32, name="raw_big")
+                raw = big.tile([P, 2, PASSES, 4, N], F32, name="raw_big", align_bytes=ALIGN)
                 nc.sync.dma_start(out=raw[:], in_=w_rows[:, e0 : e0 + 2])
                 if e0 >= SHARED_FROM:
                     units = ((e0 + 1, 0, PASSES, raw[:, 1], True), (e0, 0, PASSES, raw[:, 0], False))
                 else:
                     units = ((e0, 0, PASSES, raw[:, 0], False), (e0 + 1, 0, PASSES, raw[:, 1], False))
             else:
-                raw = small.tile([P, PASSES, 4, N], F32, name="raw_small")
+                raw = small.tile([P, PASSES, 4, N], F32, name="raw_small", align_bytes=ALIGN)
                 nc.sync.dma_start(out=raw[:], in_=w_rows[:, e0])
                 units = ((e0, 0, 2, raw[:, 0:2], True), (e0, 2, 4, raw[:, 2:4], False))
             if e0 in BIASES_BEHIND:
@@ -175,7 +176,7 @@ def tile_routed_moe_kernel(tc, xT, w, b, gate, offs, pos1, pos2, out):
             for e in sorted(set(unit[0] for unit in units)):
                 multiply(e)
         for a0, a1, on_vector in ((0, 2, False), (2, 3, True), (3, 4, False)):
-            raw = keep.tile([P, a1 - a0, 4, N], F32, name=f"raw_last{a0}")
+            raw = keep.tile([P, a1 - a0, 4, N], F32, name=f"raw_last{a0}", align_bytes=ALIGN)
             nc.sync.dma_start(out=raw[:], in_=w_rows[:, E - 1, a0:a1])
             quantise_weights(E - 1, a0, a1, raw[:], on_vector)
         biases = load_biases(done, E)
@@ -187,7 +188,7 @@ def tile_routed_moe_kernel(tc, xT, w, b, gate, offs, pos1, pos2, out):
         multiply(E - 1)
         activate(E - 1, E, biases[:, E - 1 - done : E - done])
 
-        first = keep.tile([P, T], F32, name="first")
+        first = keep.tile([P, T], F32, name="first", align_bytes=ALIGN)
         nc.vector.tensor_tensor(first[:], y[:].indirect(pos1_sb[:]), gates[:, 0], MULT)
         starts = [sum(PIECES[:i]) for i in range(len(PIECES) + 1)]
         seconds = []

@@ -15,33 +15,36 @@ MULT, ADD = mybir.AluOpType.mult, mybir.AluOpType.add
 GELU = mybir.ActivationFunctionType.Gelu_apprx_tanh
 
 P = 128
-ALIGN = 256
 PASSES = K // 512
-HALF = T // 2
 SLOTS = E * C
+HALF, QUARTER = T // 2, T // 4
+ALIGN = 256
+
 GATHERS = (768, 768, 512)
-PAIRED = 12
-SHARED_FROM = 6
-HALVED = 2
+WHOLE_ON_VECTOR = (7, 9)
+SHARED_FROM = 11
+BIASES_BEHIND = 11
 BANKED = 8
-BIASES_BEHIND = (10,)
+LAST_CUTS = ((0, 2), (2, 3), (3, 4))
 PIECES = (576, 320, 128)
+RAW_BUFS = 10
+STAGE_BUFS = 9
+WEIGHT_BUFS = 6
 
 
 def tile_routed_moe_kernel(tc, xT, w, b, gate, offs, pos1, pos2, out):
     nc = tc.nc
     with ExitStack() as ctx:
         keep = ctx.enter_context(tc.tile_pool(name="keep", bufs=1))
-        big = ctx.enter_context(tc.tile_pool(name="big", bufs=4))
-        small = ctx.enter_context(tc.tile_pool(name="small", bufs=3))
-        stage = ctx.enter_context(tc.tile_pool(name="stage", bufs=8))
-        wts = ctx.enter_context(tc.tile_pool(name="wts", bufs=6))
+        raws = ctx.enter_context(tc.tile_pool(name="raws", bufs=RAW_BUFS))
+        stage = ctx.enter_context(tc.tile_pool(name="stage", bufs=STAGE_BUFS))
+        wts = ctx.enter_context(tc.tile_pool(name="wts", bufs=WEIGHT_BUFS))
         work = ctx.enter_context(tc.tile_pool(name="work", bufs=len(PIECES)))
         psum = ctx.enter_context(tc.psum_pool(name="psum", bufs=8))
 
-        dummy = keep.tile([P, 2], F32, name="dummy")
-        nc.gpsimd.memset(dummy[:], 0.0)
-        nc.scalar.activation(dummy[:, 1:2], dummy[:, 0:1], GELU)
+        warm = keep.tile([P, 2], F32, name="warm")
+        nc.gpsimd.memset(warm[:], 0.0)
+        nc.scalar.activation(warm[:, 1:2], warm[:, 0:1], GELU)
         x_scales = keep.tile([P, T], U8, name="x_scales", align_bytes=ALIGN)
         nc.gpsimd.memset(x_scales[:], 0)
 
@@ -63,47 +66,48 @@ def tile_routed_moe_kernel(tc, xT, w, b, gate, offs, pos1, pos2, out):
                 nc.vector.tensor_copy(dst[:, s : s + width], window[:].indirect(idx))
                 s += width
 
-        def interleave(on_vector, dst, src):
+        def interleave(raw, on_vector):
+            passes, columns = raw.shape[1], raw.shape[3]
+            grouped = stage.tile([P, passes, columns, 4], BF16, name="grouped", align_bytes=ALIGN)
+            src = raw.rearrange("p a j (c i) -> p a c j i", i=4)
+            dst = grouped[:].rearrange("p a (c i) j -> p a c j i", i=4)
             if on_vector:
                 nc.vector.tensor_copy(dst, src)
             else:
                 nc.scalar.copy(dst, src)
+            return grouped[:].rearrange("p a c j -> p (a c j)")
 
-        def quantise_tokens(a, h, raw, on_vector):
-            cols = slice(h * HALF, (h + 1) * HALF)
-            grouped = stage.tile([P, HALF, 4], BF16, name="grouped", align_bytes=ALIGN)
-            interleave(
-                on_vector,
-                grouped[:].rearrange("p (c i) j -> p c j i", i=4),
-                raw.rearrange("p j (c i) -> p c j i", i=4),
-            )
-            nc.vector.quantize_mx(
-                out=x_words[a][:, cols].bitcast(FP8X4),
-                scales=x_scales[4 * a : P, cols],
-                in_=grouped[:].rearrange("p t j -> p (t j)"),
-            )
+        x_rows = xT.rearrange("(a p j) t -> p a j t", p=P, j=4)
+        for a in range(PASSES):
+            for t0 in (0, HALF):
+                raw = raws.tile([P, 1, 4, HALF], F32, name="raw", align_bytes=ALIGN)
+                nc.sync.dma_start(out=raw[:], in_=x_rows[:, a : a + 1, :, t0 : t0 + HALF])
+                width = QUARTER if a == 0 else HALF
+                for q0 in range(0, HALF, width):
+                    on_vector = a == 0 and t0 + q0 < T - QUARTER
+                    grouped = interleave(raw[:, :, :, q0 : q0 + width], on_vector)
+                    cols = slice(t0 + q0, t0 + q0 + width)
+                    nc.vector.quantize_mx(
+                        out=x_words[a][:, cols].bitcast(FP8X4), scales=x_scales[4 * a : P, cols], in_=grouped
+                    )
+            if a == 0:
+                nc.sync.dma_start(offs_sb[:], offs)
+            gather(slot_words[a], x_words[a])
+        gather(slot_scales, x_scales)
 
-        weights = {}
+        w_rows = w.rearrange("e (a p j) n -> e p a j n", p=P, j=4)
+        weights, sums = {}, {}
 
-        def quantise_weights(e, a0, a1, raw, on_vector):
+        def quantise_weights(e, parts):
             if e not in weights:
-                w_words = wts.tile([P, PASSES, N], U32, name="w_words", align_bytes=ALIGN)
-                w_scales = wts.tile([P, PASSES, N], U8, name="w_scales", align_bytes=ALIGN)
+                w_words = wts.tile([P, PASSES * N], U32, name="w_words", align_bytes=ALIGN)
+                w_scales = wts.tile([P, PASSES * N], U8, name="w_scales", align_bytes=ALIGN)
                 weights[e] = (w_words, w_scales)
             w_words, w_scales = weights[e]
-            grouped = stage.tile([P, a1 - a0, N, 4], BF16, name="grouped", align_bytes=ALIGN)
-            interleave(
-                on_vector,
-                grouped[:].rearrange("p a (c i) j -> p a c j i", i=4),
-                raw.rearrange("p a j (c i) -> p a c j i", i=4),
-            )
-            nc.vector.quantize_mx(
-                out=w_words[:, a0:a1].rearrange("p a n -> p (a n)").bitcast(FP8X4),
-                scales=w_scales[:, a0:a1].rearrange("p a n -> p (a n)"),
-                in_=grouped[:].rearrange("p a n j -> p (a n j)"),
-            )
-
-        sums = {}
+            copied = [(a0, raw.shape[1], interleave(raw, on_vector)) for a0, raw, on_vector in parts]
+            for a0, passes, grouped in copied:
+                cols = slice(a0 * N, (a0 + passes) * N)
+                nc.vector.quantize_mx(out=w_words[:, cols].bitcast(FP8X4), scales=w_scales[:, cols], in_=grouped)
 
         def multiply(e):
             w_words, w_scales = weights[e]
@@ -115,10 +119,11 @@ def tile_routed_moe_kernel(tc, xT, w, b, gate, offs, pos1, pos2, out):
                     sums[e + i] = bank[:, i]
             slots = slice(e * C, (e + 1) * C)
             for a in range(PASSES):
+                cols = slice(a * N, (a + 1) * N)
                 nc.tensor.matmul_mx(
                     out=sums[e][:],
-                    lhsT=w_words[:, a].bitcast(FP8X4),
-                    lhsT_scale=w_scales[:, a],
+                    lhsT=w_words[:, cols].bitcast(FP8X4),
+                    lhsT_scale=w_scales[:, cols],
                     rhs=slot_words[a][:, slots].bitcast(FP8X4),
                     rhs_scale=slot_scales[4 * a : P, slots],
                     start=(a == 0),
@@ -126,67 +131,40 @@ def tile_routed_moe_kernel(tc, xT, w, b, gate, offs, pos1, pos2, out):
                 )
 
         def load_biases(e0, e1):
-            biases = keep.tile([P, e1 - e0], F32, name=f"biases{e0}")
-            nc.sync.dma_start(biases[:], b[:, e0:e1])
-            return biases
+            tile = keep.tile([P, e1 - e0], F32, name=f"biases{e0}")
+            nc.sync.dma_start(tile[:], b[:, e0:e1])
+            return {e: tile[:, e - e0 : e - e0 + 1] for e in range(e0, e1)}
 
-        def activate(e0, e1, biases):
-            for e in range(e0, e1):
-                nc.scalar.activation(y[:, e * C : (e + 1) * C], sums[e][:], GELU, bias=biases[:, e - e0 : e - e0 + 1])
+        def activate(e, bias):
+            nc.scalar.activation(y[:, e * C : (e + 1) * C], sums[e][:], GELU, bias=bias)
 
-        x_rows = xT.rearrange("(a p j) t -> a p j t", p=P, j=4)
-        for a in range(PASSES):
-            if a >= HALVED:
-                raw = big.tile([P, 4, T], F32, name="raw_big", align_bytes=ALIGN)
-                nc.sync.dma_start(out=raw[:], in_=x_rows[a])
-            for h in range(2):
-                cols = slice(h * HALF, (h + 1) * HALF)
-                if a < HALVED:
-                    half = small.tile([P, 4, HALF], F32, name="raw_small", align_bytes=ALIGN)
-                    nc.sync.dma_start(out=half[:], in_=x_rows[a, :, :, cols])
-                    quantise_tokens(a, h, half[:], a == 0)
-                else:
-                    quantise_tokens(a, h, raw[:, :, cols], False)
-            if a == 0:
-                nc.sync.dma_start(offs_sb[:], offs)
-            gather(slot_words[a], x_words[a])
-        gather(slot_scales, x_scales)
-
-        w_rows = w.rearrange("e (a p j) n -> p e a j n", p=P, j=4)
-        done = 0
-        for e0 in list(range(0, PAIRED, 2)) + list(range(PAIRED, E - 1)):
-            if e0 < PAIRED:
-                raw = big.tile([P, 2, PASSES, 4, N], F32, name="raw_big", align_bytes=ALIGN)
-                nc.sync.dma_start(out=raw[:], in_=w_rows[:, e0 : e0 + 2])
-                if e0 >= SHARED_FROM:
-                    units = ((e0 + 1, 0, PASSES, raw[:, 1], True), (e0, 0, PASSES, raw[:, 0], False))
-                else:
-                    units = ((e0, 0, PASSES, raw[:, 0], False), (e0 + 1, 0, PASSES, raw[:, 1], False))
+        for e in range(E - 1):
+            raw = raws.tile([P, PASSES, 4, N], F32, name="raw", align_bytes=ALIGN)
+            nc.sync.dma_start(out=raw[:], in_=w_rows[e])
+            if e == BIASES_BEHIND:
+                biases = load_biases(0, e)
+            if e >= SHARED_FROM or e in WHOLE_ON_VECTOR:
+                quantise_weights(e, [(0, raw[:, 0:2], True), (2, raw[:, 2:4], e < SHARED_FROM)])
             else:
-                raw = small.tile([P, PASSES, 4, N], F32, name="raw_small", align_bytes=ALIGN)
-                nc.sync.dma_start(out=raw[:], in_=w_rows[:, e0])
-                units = ((e0, 0, 2, raw[:, 0:2], True), (e0, 2, 4, raw[:, 2:4], False))
-            if e0 in BIASES_BEHIND:
-                biases = load_biases(done, e0)
-            for unit in units:
-                quantise_weights(*unit)
-            if e0 in BIASES_BEHIND:
-                activate(done, e0, biases)
-                done = e0
-            for e in sorted(set(unit[0] for unit in units)):
-                multiply(e)
-        for a0, a1, on_vector in ((0, 2, False), (2, 3, True), (3, 4, False)):
+                quantise_weights(e, [(0, raw[:], False)])
+            if e == BIASES_BEHIND:
+                for done in range(e):
+                    activate(done, biases[done])
+            multiply(e)
+        for a0, a1 in LAST_CUTS:
             raw = keep.tile([P, a1 - a0, 4, N], F32, name=f"raw_last{a0}", align_bytes=ALIGN)
-            nc.sync.dma_start(out=raw[:], in_=w_rows[:, E - 1, a0:a1])
-            quantise_weights(E - 1, a0, a1, raw[:], on_vector)
-        biases = load_biases(done, E)
+            nc.sync.dma_start(out=raw[:], in_=w_rows[E - 1, :, a0:a1])
+            quantise_weights(E - 1, [(a, raw[:, a - a0 : a - a0 + 1], a == 0) for a in range(a0, a1)])
+
+        biases = load_biases(BIASES_BEHIND, E)
         nc.sync.dma_start(pos1_sb[:], pos1)
         nc.sync.dma_start(gates[:, 0], gate[0])
         nc.sync.dma_start(pos2_sb[:], pos2)
         nc.sync.dma_start(gates[:, 1], gate[1])
-        activate(done, E - 1, biases)
+        for e in range(BIASES_BEHIND, E - 1):
+            activate(e, biases[e])
         multiply(E - 1)
-        activate(E - 1, E, biases[:, E - 1 - done : E - done])
+        activate(E - 1, biases[E - 1])
 
         first = keep.tile([P, T], F32, name="first", align_bytes=ALIGN)
         nc.vector.tensor_tensor(first[:], y[:].indirect(pos1_sb[:]), gates[:, 0], MULT)
@@ -194,14 +172,12 @@ def tile_routed_moe_kernel(tc, xT, w, b, gate, offs, pos1, pos2, out):
         seconds = []
         for i in range(len(PIECES) + 1):
             if i < len(PIECES):
-                idx = slice(starts[i] // 16, starts[i + 1] // 16)
-                second = work.tile([P, PIECES[i]], F32, name="second")
-                nc.vector.tensor_tensor(
-                    second[:], y[:].indirect(pos2_sb[:, idx]), gates[:, 1, starts[i] : starts[i + 1]], MULT
-                )
+                idx = pos2_sb[:, starts[i] // 16 : starts[i + 1] // 16]
+                second = work.tile([P, PIECES[i]], F32, name="second", align_bytes=ALIGN)
+                nc.vector.tensor_tensor(second[:], y[:].indirect(idx), gates[:, 1, starts[i] : starts[i + 1]], MULT)
                 seconds.append(second)
             if i > 0:
                 cols = slice(starts[i - 1], starts[i])
-                total = work.tile([P, PIECES[i - 1]], F32, name="total")
+                total = work.tile([P, PIECES[i - 1]], F32, name="total", align_bytes=ALIGN)
                 nc.vector.tensor_tensor(total[:], first[:, cols], seconds[i - 1][:], ADD)
                 nc.sync.dma_start(out=out[:, cols], in_=total[:])

@@ -66,15 +66,16 @@ def tile_routed_moe_kernel(tc, xT, w, b, gate, offs, pos1, pos2, out):
                 nc.vector.tensor_copy(dst[:, s : s + width], window[:].indirect(idx))
                 s += width
 
-        def interleave(raw, on_vector):
+        def interleave(raw, share):
             passes, columns = raw.shape[1], raw.shape[3]
             grouped = stage.tile([P, passes, columns, 4], BF16, name="grouped", align_bytes=ALIGN)
             src = raw.rearrange("p a j (c i) -> p a c j i", i=4)
             dst = grouped[:].rearrange("p a (c i) j -> p a c j i", i=4)
-            if on_vector:
-                nc.vector.tensor_copy(dst, src)
-            else:
-                nc.scalar.copy(dst, src)
+            cut = int(share * columns) // 4
+            if cut > 0:
+                nc.vector.tensor_copy(dst[:, :, 0:cut], src[:, :, 0:cut])
+            if cut < columns // 4:
+                nc.scalar.copy(dst[:, :, cut:], src[:, :, cut:])
             return grouped[:].rearrange("p a c j -> p (a c j)")
 
         x_rows = xT.rearrange("(a p j) t -> p a j t", p=P, j=4)
@@ -104,7 +105,7 @@ def tile_routed_moe_kernel(tc, xT, w, b, gate, offs, pos1, pos2, out):
                 w_scales = wts.tile([P, PASSES * N], U8, name="w_scales", align_bytes=ALIGN)
                 weights[e] = (w_words, w_scales)
             w_words, w_scales = weights[e]
-            copied = [(a0, raw.shape[1], interleave(raw, on_vector)) for a0, raw, on_vector in parts]
+            copied = [(a0, raw.shape[1], interleave(raw, share)) for a0, raw, share in parts]
             for a0, passes, grouped in copied:
                 cols = slice(a0 * N, (a0 + passes) * N)
                 nc.vector.quantize_mx(out=w_words[:, cols].bitcast(FP8X4), scales=w_scales[:, cols], in_=grouped)
@@ -154,7 +155,7 @@ def tile_routed_moe_kernel(tc, xT, w, b, gate, offs, pos1, pos2, out):
         for a0, a1 in LAST_CUTS:
             raw = keep.tile([P, a1 - a0, 4, N], F32, name=f"raw_last{a0}", align_bytes=ALIGN)
             nc.sync.dma_start(out=raw[:], in_=w_rows[E - 1, :, a0:a1])
-            quantise_weights(E - 1, [(a, raw[:, a - a0 : a - a0 + 1], a == 0) for a in range(a0, a1)])
+            quantise_weights(E - 1, [(a, raw[:, a - a0 : a - a0 + 1], (1, 0, 0, 0.625)[a]) for a in range(a0, a1)])
 
         biases = load_biases(BIASES_BEHIND, E)
         nc.sync.dma_start(pos1_sb[:], pos1)

@@ -20,14 +20,15 @@ SLOTS = E * C
 HALF, QUARTER = T // 2, T // 4
 ALIGN = 256
 
-GATHERS = (768, 768, 512)
+WINDOW = 2 * SLOTS
 WHOLE_ON_VECTOR = (7, 9)
 SHARED_FROM = 11
 BIASES_BEHIND = 11
 BANKED = 8
 LAST_CUTS = ((0, 2), (2, 3), (3, 4))
 PIECES = (576, 320, 128)
-RAW_BUFS = 10
+RAW_SLOT = PASSES * 4 * N * 4
+RAW_SLOTS = 10
 STAGE_BUFS = 9
 WEIGHT_BUFS = 6
 
@@ -36,17 +37,16 @@ def tile_routed_moe_kernel(tc, xT, w, b, gate, offs, pos1, pos2, out):
     nc = tc.nc
     with ExitStack() as ctx:
         keep = ctx.enter_context(tc.tile_pool(name="keep", bufs=1))
-        raws = ctx.enter_context(tc.tile_pool(name="raws", bufs=RAW_BUFS))
+        raws = ctx.enter_context(tc.tile_pool(name="raws", bufs=1))
         stage = ctx.enter_context(tc.tile_pool(name="stage", bufs=STAGE_BUFS))
         wts = ctx.enter_context(tc.tile_pool(name="wts", bufs=WEIGHT_BUFS))
-        work = ctx.enter_context(tc.tile_pool(name="work", bufs=len(PIECES)))
         psum = ctx.enter_context(tc.psum_pool(name="psum", bufs=8))
 
         warm = keep.tile([P, 2], F32, name="warm")
         nc.gpsimd.memset(warm[:], 0.0)
         nc.scalar.activation(warm[:, 1:2], warm[:, 0:1], GELU)
-        x_scales = keep.tile([P, T], U8, name="x_scales", align_bytes=ALIGN)
-        nc.gpsimd.memset(x_scales[:], 0)
+        x_scales = keep.tile([P, WINDOW], U8, name="x_scales", align_bytes=ALIGN)
+        nc.gpsimd.memset(x_scales[:, 0:T], 0)
 
         offs_sb = keep.tile([P, SLOTS // 16], U16, name="offs_sb")
         pos1_sb = keep.tile([P, T // 16], U16, name="pos1_sb")
@@ -54,17 +54,12 @@ def tile_routed_moe_kernel(tc, xT, w, b, gate, offs, pos1, pos2, out):
         y = keep.tile([P, SLOTS], F32, name="y", align_bytes=ALIGN)
         gates = keep.tile([P, 2, T], F32, name="gates", align_bytes=ALIGN)
         slot_scales = keep.tile([P, SLOTS], U8, name="slot_scales", align_bytes=ALIGN)
+        all_words = keep.tile([P, (PASSES - 1) * T + WINDOW], U32, name="all_words", align_bytes=ALIGN)
         x_words, slot_words = [], []
         for a in range(PASSES):
-            x_words.append(keep.tile([P, T], U32, name=f"x_words{a}", align_bytes=ALIGN))
+            start = (PASSES - 1 - a) * T
+            x_words.append(all_words[:, start : start + WINDOW])
             slot_words.append(keep.tile([P, SLOTS], U32, name=f"slot_words{a}", align_bytes=ALIGN))
-
-        def gather(dst, window):
-            s = 0
-            for width in GATHERS:
-                idx = offs_sb[:, s // 16 : (s + width) // 16]
-                nc.vector.tensor_copy(dst[:, s : s + width], window[:].indirect(idx))
-                s += width
 
         def interleave(raw, share):
             passes, columns = raw.shape[1], raw.shape[3]
@@ -80,21 +75,19 @@ def tile_routed_moe_kernel(tc, xT, w, b, gate, offs, pos1, pos2, out):
 
         x_rows = xT.rearrange("(a p j) t -> p a j t", p=P, j=4)
         for a in range(PASSES):
-            for t0 in (0, HALF):
-                raw = raws.tile([P, 1, 4, HALF], F32, name="raw", align_bytes=ALIGN)
-                nc.sync.dma_start(out=raw[:], in_=x_rows[:, a : a + 1, :, t0 : t0 + HALF])
-                width = QUARTER if a == 0 else HALF
-                for q0 in range(0, HALF, width):
-                    on_vector = a == 0 and t0 + q0 < T - QUARTER
-                    grouped = interleave(raw[:, :, :, q0 : q0 + width], on_vector)
-                    cols = slice(t0 + q0, t0 + q0 + width)
-                    nc.vector.quantize_mx(
-                        out=x_words[a][:, cols].bitcast(FP8X4), scales=x_scales[4 * a : P, cols], in_=grouped
-                    )
+            raw = raws.tile([P, 1, 4, T], F32, name=f"raw_x{a}", align_bytes=ALIGN, offset=2 * a * RAW_SLOT)
+            nc.sync.dma_start(out=raw[:], in_=x_rows[:, a : a + 1])
+            width = QUARTER if a == 0 else HALF
+            for t0 in range(0, T, width):
+                grouped = interleave(raw[:, :, :, t0 : t0 + width], a == 0 and t0 < HALF)
+                cols = slice(t0, t0 + width)
+                nc.vector.quantize_mx(
+                    out=x_words[a][:, cols].bitcast(FP8X4), scales=x_scales[4 * a : P, cols], in_=grouped
+                )
             if a == 0:
                 nc.sync.dma_start(offs_sb[:], offs)
-            gather(slot_words[a], x_words[a])
-        gather(slot_scales, x_scales)
+            nc.vector.tensor_copy(slot_words[a][:], x_words[a].indirect(offs_sb[:]))
+        nc.vector.tensor_copy(slot_scales[:], x_scales[:].indirect(offs_sb[:]))
 
         w_rows = w.rearrange("e (a p j) n -> e p a j n", p=P, j=4)
         weights, sums = {}, {}
@@ -140,7 +133,8 @@ def tile_routed_moe_kernel(tc, xT, w, b, gate, offs, pos1, pos2, out):
             nc.scalar.activation(y[:, e * C : (e + 1) * C], sums[e][:], GELU, bias=bias)
 
         for e in range(E - 1):
-            raw = raws.tile([P, PASSES, 4, N], F32, name="raw", align_bytes=ALIGN)
+            place = (2 * PASSES + e) % RAW_SLOTS * RAW_SLOT
+            raw = raws.tile([P, PASSES, 4, N], F32, name=f"raw_w{e}", align_bytes=ALIGN, offset=place)
             nc.sync.dma_start(out=raw[:], in_=w_rows[e])
             if e == BIASES_BEHIND:
                 biases = load_biases(0, e)
@@ -174,11 +168,11 @@ def tile_routed_moe_kernel(tc, xT, w, b, gate, offs, pos1, pos2, out):
         for i in range(len(PIECES) + 1):
             if i < len(PIECES):
                 idx = pos2_sb[:, starts[i] // 16 : starts[i + 1] // 16]
-                second = work.tile([P, PIECES[i]], F32, name="second", align_bytes=ALIGN)
+                second = keep.tile([P, PIECES[i]], F32, name=f"second{i}", align_bytes=ALIGN)
                 nc.vector.tensor_tensor(second[:], y[:].indirect(idx), gates[:, 1, starts[i] : starts[i + 1]], MULT)
                 seconds.append(second)
             if i > 0:
                 cols = slice(starts[i - 1], starts[i])
-                total = work.tile([P, PIECES[i - 1]], F32, name="total", align_bytes=ALIGN)
+                total = keep.tile([P, PIECES[i - 1]], F32, name=f"total{i}", align_bytes=ALIGN)
                 nc.vector.tensor_tensor(total[:], first[:, cols], seconds[i - 1][:], ADD)
                 nc.sync.dma_start(out=out[:, cols], in_=total[:])

@@ -1,6 +1,7 @@
 from contextlib import ExitStack
 
 import concourse.mybir as mybir
+from concourse.masks import make_identity
 
 K, T, E, C, N = 2048, 1024, 16, 128, 128
 FLOPS = 2 * K * E * C * N
@@ -26,11 +27,14 @@ SHARED_FROM = 11
 BIASES_BEHIND = 11
 BANKED = 8
 LAST_CUTS = ((0, 2), (2, 3), (3, 4))
-PIECES = (576, 320, 128)
+VECTOR_CUTS = (512, 768, 896, 1024)
+TENSOR_CUTS = (0, 256, 512)
+ON_TENSOR = TENSOR_CUTS[-1]
 RAW_SLOT = PASSES * 4 * N * 4
 RAW_SLOTS = 10
+PAIRED = 4
 STAGE_BUFS = 9
-WEIGHT_BUFS = 6
+WEIGHT_BUFS = 5
 
 
 def tile_routed_moe_kernel(tc, xT, w, b, gate, offs, pos1, pos2, out):
@@ -47,6 +51,9 @@ def tile_routed_moe_kernel(tc, xT, w, b, gate, offs, pos1, pos2, out):
         nc.scalar.activation(warm[:, 1:2], warm[:, 0:1], GELU)
         x_scales = keep.tile([P, WINDOW], U8, name="x_scales", align_bytes=ALIGN)
         nc.gpsimd.memset(x_scales[:, 0:T], 0)
+
+        identity = keep.tile([P, P], F32, name="identity", align_bytes=ALIGN)
+        make_identity(nc, identity[:])
 
         offs_sb = keep.tile([P, SLOTS // 16], U16, name="offs_sb")
         pos1_sb = keep.tile([P, T // 16], U16, name="pos1_sb")
@@ -89,7 +96,7 @@ def tile_routed_moe_kernel(tc, xT, w, b, gate, offs, pos1, pos2, out):
             nc.vector.tensor_copy(slot_words[a][:], x_words[a].indirect(offs_sb[:]))
         nc.vector.tensor_copy(slot_scales[:], x_scales[:].indirect(offs_sb[:]))
 
-        w_rows = w.rearrange("e (a p j) n -> e p a j n", p=P, j=4)
+        w_rows = w.rearrange("e (a p j) n -> p (e a) j n", p=P, j=4)
         weights, sums = {}, {}
 
         def quantise_weights(e, parts):
@@ -133,46 +140,60 @@ def tile_routed_moe_kernel(tc, xT, w, b, gate, offs, pos1, pos2, out):
             nc.scalar.activation(y[:, e * C : (e + 1) * C], sums[e][:], GELU, bias=bias)
 
         for e in range(E - 1):
-            place = (2 * PASSES + e) % RAW_SLOTS * RAW_SLOT
-            raw = raws.tile([P, PASSES, 4, N], F32, name=f"raw_w{e}", align_bytes=ALIGN, offset=place)
-            nc.sync.dma_start(out=raw[:], in_=w_rows[e])
+            if e >= PAIRED or e % 2 == 0:
+                count = 2 if e < PAIRED else 1
+                place = (2 * PASSES + e) % RAW_SLOTS * RAW_SLOT
+                loaded = raws.tile([P, count * PASSES, 4, N], F32, name=f"raw_w{e}", align_bytes=ALIGN, offset=place)
+                nc.sync.dma_start(out=loaded[:], in_=w_rows[:, e * PASSES : (e + count) * PASSES])
+                first_loaded = e
+            raw = loaded[:, (e - first_loaded) * PASSES : (e - first_loaded + 1) * PASSES]
             if e == BIASES_BEHIND:
                 biases = load_biases(0, e)
             if e >= SHARED_FROM or e in WHOLE_ON_VECTOR:
                 quantise_weights(e, [(0, raw[:, 0:2], True), (2, raw[:, 2:4], e < SHARED_FROM)])
             else:
-                quantise_weights(e, [(0, raw[:], False)])
+                quantise_weights(e, [(0, raw, False)])
             if e == BIASES_BEHIND:
                 for done in range(e):
                     activate(done, biases[done])
             multiply(e)
         for a0, a1 in LAST_CUTS:
             raw = keep.tile([P, a1 - a0, 4, N], F32, name=f"raw_last{a0}", align_bytes=ALIGN)
-            nc.sync.dma_start(out=raw[:], in_=w_rows[E - 1, :, a0:a1])
+            nc.sync.dma_start(out=raw[:], in_=w_rows[:, (E - 1) * PASSES + a0 : (E - 1) * PASSES + a1])
             quantise_weights(E - 1, [(a, raw[:, a - a0 : a - a0 + 1], (1, 0, 0, 0.625)[a]) for a in range(a0, a1)])
 
         biases = load_biases(BIASES_BEHIND, E)
         nc.sync.dma_start(pos1_sb[:], pos1)
-        nc.sync.dma_start(gates[:, 0], gate[0])
         nc.sync.dma_start(pos2_sb[:], pos2)
-        nc.sync.dma_start(gates[:, 1], gate[1])
+        for t0 in (0, HALF):
+            nc.sync.dma_start(gates[:, :, t0 : t0 + HALF], gate[:, :, t0 : t0 + HALF].rearrange("r n t -> n r t"))
         for e in range(BIASES_BEHIND, E - 1):
             activate(e, biases[e])
         multiply(E - 1)
         activate(E - 1, biases[E - 1])
 
-        first = keep.tile([P, T], F32, name="first", align_bytes=ALIGN)
-        nc.vector.tensor_tensor(first[:], y[:].indirect(pos1_sb[:]), gates[:, 0], MULT)
-        starts = [sum(PIECES[:i]) for i in range(len(PIECES) + 1)]
+        def gated(name, pos_sb, which, t0, t1):
+            tile = keep.tile([P, t1 - t0], F32, name=name, align_bytes=ALIGN)
+            idx = pos_sb[:, t0 // 16 : t1 // 16]
+            nc.vector.tensor_tensor(tile[:], y[:].indirect(idx), gates[:, which, t0:t1], MULT)
+            return tile
+
+        added = keep.tile([P, ON_TENSOR], F32, name="added", align_bytes=ALIGN)
+        for t0, t1 in zip(TENSOR_CUTS, TENSOR_CUTS[1:]):
+            bank = psum.tile([P, t1 - t0], F32, name="sums")
+            nc.tensor.matmul(bank[:], identity[:], gated(f"first{t0}", pos1_sb, 0, t0, t1)[:], start=True, stop=False)
+            nc.tensor.matmul(bank[:], identity[:], gated(f"second{t0}", pos2_sb, 1, t0, t1)[:], start=False, stop=True)
+            nc.scalar.copy(added[:, t0:t1], bank[:])
+            nc.scalar.dma_start(out=out[:, t0:t1], in_=added[:, t0:t1])
+        first = gated("first", pos1_sb, 0, ON_TENSOR, T)
+        pieces = list(zip(VECTOR_CUTS, VECTOR_CUTS[1:]))
         seconds = []
-        for i in range(len(PIECES) + 1):
-            if i < len(PIECES):
-                idx = pos2_sb[:, starts[i] // 16 : starts[i + 1] // 16]
-                second = keep.tile([P, PIECES[i]], F32, name=f"second{i}", align_bytes=ALIGN)
-                nc.vector.tensor_tensor(second[:], y[:].indirect(idx), gates[:, 1, starts[i] : starts[i + 1]], MULT)
-                seconds.append(second)
+        for i in range(len(pieces) + 1):
+            if i < len(pieces):
+                t0, t1 = pieces[i]
+                seconds.append(gated(f"second{t0}", pos2_sb, 1, t0, t1))
             if i > 0:
-                cols = slice(starts[i - 1], starts[i])
-                total = keep.tile([P, PIECES[i - 1]], F32, name=f"total{i}", align_bytes=ALIGN)
-                nc.vector.tensor_tensor(total[:], first[:, cols], seconds[i - 1][:], ADD)
-                nc.sync.dma_start(out=out[:, cols], in_=total[:])
+                t0, t1 = pieces[i - 1]
+                total = keep.tile([P, t1 - t0], F32, name=f"total{t0}", align_bytes=ALIGN)
+                nc.vector.tensor_tensor(total[:], first[:, t0 - ON_TENSOR : t1 - ON_TENSOR], seconds[i - 1][:], ADD)
+                nc.sync.dma_start(out=out[:, t0:t1], in_=total[:])

@@ -25,6 +25,7 @@ WINDOW = 2 * SLOTS
 WHOLE_ON_VECTOR = (7, 9)
 SHARED_FROM = 11
 BIASES_BEHIND = 11
+EARLY_GELUS = 8
 BANKED = 8
 LAST_CUTS = ((0, 2), (2, 3), (3, 4))
 VECTOR_CUTS = (512, 768, 896, 1024)
@@ -148,26 +149,26 @@ def tile_routed_moe_kernel(tc, xT, w, b, gate, offs, pos1, pos2, out):
                 first_loaded = e
             raw = loaded[:, (e - first_loaded) * PASSES : (e - first_loaded + 1) * PASSES]
             if e == BIASES_BEHIND:
-                biases = load_biases(0, e)
+                biases = load_biases(0, EARLY_GELUS)
             if e >= SHARED_FROM or e in WHOLE_ON_VECTOR:
                 quantise_weights(e, [(0, raw[:, 0:2], True), (2, raw[:, 2:4], e < SHARED_FROM)])
             else:
                 quantise_weights(e, [(0, raw, False)])
             if e == BIASES_BEHIND:
-                for done in range(e):
+                for done in range(EARLY_GELUS):
                     activate(done, biases[done])
             multiply(e)
         for a0, a1 in LAST_CUTS:
             raw = keep.tile([P, a1 - a0, 4, N], F32, name=f"raw_last{a0}", align_bytes=ALIGN)
             nc.sync.dma_start(out=raw[:], in_=w_rows[:, (E - 1) * PASSES + a0 : (E - 1) * PASSES + a1])
-            quantise_weights(E - 1, [(a, raw[:, a - a0 : a - a0 + 1], (1, 0, 0, 0.625)[a]) for a in range(a0, a1)])
+            quantise_weights(E - 1, [(a, raw[:, a - a0 : a - a0 + 1], (1, 0, 0, 1)[a]) for a in range(a0, a1)])
 
-        biases = load_biases(BIASES_BEHIND, E)
+        biases = load_biases(EARLY_GELUS, E)
         nc.sync.dma_start(pos1_sb[:], pos1)
         nc.sync.dma_start(pos2_sb[:], pos2)
         for t0 in (0, HALF):
             nc.sync.dma_start(gates[:, :, t0 : t0 + HALF], gate[:, :, t0 : t0 + HALF].rearrange("r n t -> n r t"))
-        for e in range(BIASES_BEHIND, E - 1):
+        for e in range(EARLY_GELUS, E - 1):
             activate(e, biases[e])
         multiply(E - 1)
         activate(E - 1, biases[E - 1])

@@ -28,12 +28,12 @@ BIASES_BEHIND = 11
 EARLY_GELUS = 8
 BANKED = 8
 LAST_CUTS = ((0, 2), (2, 3), (3, 4))
-VECTOR_CUTS = (512, 768, 896, 1024)
-TENSOR_CUTS = (0, 256, 512)
+VECTOR_CUTS = (448, 704, 896, 1024)
+TENSOR_CUTS = (0, 256, 448)
 ON_TENSOR = TENSOR_CUTS[-1]
 RAW_SLOT = PASSES * 4 * N * 4
 RAW_SLOTS = 10
-PAIRED = 4
+PAIRED = 6
 STAGE_BUFS = 9
 WEIGHT_BUFS = 5
 
@@ -140,7 +140,7 @@ def tile_routed_moe_kernel(tc, xT, w, b, gate, offs, pos1, pos2, out):
         def activate(e, bias):
             nc.scalar.activation(y[:, e * C : (e + 1) * C], sums[e][:], GELU, bias=bias)
 
-        for e in range(E - 1):
+        for e in range(E - 2):
             if e >= PAIRED or e % 2 == 0:
                 count = 2 if e < PAIRED else 1
                 place = (2 * PASSES + e) % RAW_SLOTS * RAW_SLOT
@@ -158,6 +158,12 @@ def tile_routed_moe_kernel(tc, xT, w, b, gate, offs, pos1, pos2, out):
                 for done in range(EARLY_GELUS):
                     activate(done, biases[done])
             multiply(e)
+        for a0 in (0, 2):
+            place = (2 * PASSES + E - 2) % RAW_SLOTS * RAW_SLOT + a0 * (RAW_SLOT // PASSES)
+            raw = raws.tile([P, 2, 4, N], F32, name=f"raw_before_last{a0}", align_bytes=ALIGN, offset=place)
+            nc.sync.dma_start(out=raw[:], in_=w_rows[:, (E - 2) * PASSES + a0 : (E - 2) * PASSES + a0 + 2])
+            quantise_weights(E - 2, [(a0, raw[:, 0:1], 1), (a0 + 1, raw[:, 1:2], 0)])
+        multiply(E - 2)
         for a0, a1 in LAST_CUTS:
             raw = keep.tile([P, a1 - a0, 4, N], F32, name=f"raw_last{a0}", align_bytes=ALIGN)
             nc.sync.dma_start(out=raw[:], in_=w_rows[:, (E - 1) * PASSES + a0 : (E - 1) * PASSES + a1])

@@ -28,8 +28,8 @@ BIASES_BEHIND = 11
 EARLY_GELUS = 8
 BANKED = 8
 LAST_CUTS = ((0, 2), (2, 3), (3, 4))
-VECTOR_CUTS = (448, 704, 896, 1024)
-TENSOR_CUTS = (0, 256, 448)
+VECTOR_CUTS = (512, 768, 896, 1024)
+TENSOR_CUTS = (0, 256, 512)
 ON_TENSOR = TENSOR_CUTS[-1]
 RAW_SLOT = PASSES * 4 * N * 4
 RAW_SLOTS = 10
@@ -186,12 +186,26 @@ def tile_routed_moe_kernel(tc, xT, w, b, gate, offs, pos1, pos2, out):
             return tile
 
         added = keep.tile([P, ON_TENSOR], F32, name="added", align_bytes=ALIGN)
-        for t0, t1 in zip(TENSOR_CUTS, TENSOR_CUTS[1:]):
-            bank = psum.tile([P, t1 - t0], F32, name="sums")
-            nc.tensor.matmul(bank[:], identity[:], gated(f"first{t0}", pos1_sb, 0, t0, t1)[:], start=True, stop=False)
-            nc.tensor.matmul(bank[:], identity[:], gated(f"second{t0}", pos2_sb, 1, t0, t1)[:], start=False, stop=True)
-            nc.scalar.copy(added[:, t0:t1], bank[:])
-            nc.scalar.dma_start(out=out[:, t0:t1], in_=added[:, t0:t1])
+        c1 = TENSOR_CUTS[1]
+        blocks = [slice(c, c + P) for c in range(0, c1, P)]
+        turned = [psum.tile([P, P], F32, name="sums") for block in blocks]
+        for which, pos_sb in enumerate((pos1_sb, pos2_sb)):
+            product = gated(f"turn{which}", pos_sb, which, 0, c1)
+            for bank, block in zip(turned, blocks):
+                nc.tensor.matmul(bank[:], product[:, block], identity[:], start=which == 0, stop=which == 1, is_transpose=True)
+        turned_sb = keep.tile([P, c1], F32, name="turned", align_bytes=ALIGN)
+        for bank, block in zip(turned, blocks):
+            nc.scalar.copy(turned_sb[:, block], bank[:])
+        bank = psum.tile([P, ON_TENSOR - c1], F32, name="sums")
+        nc.tensor.matmul(bank[:], identity[:], gated("first1", pos1_sb, 0, c1, ON_TENSOR)[:], start=True, stop=False)
+        back = psum.tile([P, c1], F32, name="sums")
+        for block in blocks:
+            nc.tensor.transpose(back[:, block], turned_sb[:, block], identity[:])
+        nc.scalar.copy(added[:, 0:c1], back[:])
+        nc.scalar.dma_start(out=out[:, 0:c1], in_=added[:, 0:c1])
+        nc.tensor.matmul(bank[:], identity[:], gated("second1", pos2_sb, 1, c1, ON_TENSOR)[:], start=False, stop=True)
+        nc.scalar.copy(added[:, c1:ON_TENSOR], bank[:])
+        nc.scalar.dma_start(out=out[:, c1:ON_TENSOR], in_=added[:, c1:ON_TENSOR])
         first = gated("first", pos1_sb, 0, ON_TENSOR, T)
         pieces = list(zip(VECTOR_CUTS, VECTOR_CUTS[1:]))
         seconds = []

@@ -1,7 +1,6 @@
 from contextlib import ExitStack
 
 import concourse.mybir as mybir
-from concourse.masks import make_identity
 
 K, T, E, C, N = 2048, 1024, 16, 128, 128
 FLOPS = 2 * K * E * C * N
@@ -14,6 +13,7 @@ U8 = mybir.dt.uint8
 FP8X4 = mybir.dt.float8_e4m3fn_x4
 MULT, ADD = mybir.AluOpType.mult, mybir.AluOpType.add
 GELU = mybir.ActivationFunctionType.Gelu_apprx_tanh
+COPY = mybir.ActivationFunctionType.Copy
 
 P = 128
 PASSES = K // 512
@@ -28,12 +28,11 @@ BIASES_BEHIND = 11
 EARLY_GELUS = 8
 BANKED = 8
 LAST_CUTS = ((0, 2), (2, 3), (3, 4))
-VECTOR_CUTS = (512, 768, 896, 1024)
-TENSOR_CUTS = (0, 256, 512)
-ON_TENSOR = TENSOR_CUTS[-1]
+BOTH = 384
+PIECES = ((BOTH, 640), (640, 896), (896, T))
 RAW_SLOT = PASSES * 4 * N * 4
 RAW_SLOTS = 10
-PAIRED = 6
+PAIRED = 8
 STAGE_BUFS = 9
 WEIGHT_BUFS = 5
 
@@ -52,9 +51,6 @@ def tile_routed_moe_kernel(tc, xT, w, b, gate, offs, pos1, pos2, out):
         nc.scalar.activation(warm[:, 1:2], warm[:, 0:1], GELU)
         x_scales = keep.tile([P, WINDOW], U8, name="x_scales", align_bytes=ALIGN)
         nc.gpsimd.memset(x_scales[:, 0:T], 0)
-
-        identity = keep.tile([P, P], F32, name="identity", align_bytes=ALIGN)
-        make_identity(nc, identity[:])
 
         offs_sb = keep.tile([P, SLOTS // 16], U16, name="offs_sb")
         pos1_sb = keep.tile([P, T // 16], U16, name="pos1_sb")
@@ -172,49 +168,39 @@ def tile_routed_moe_kernel(tc, xT, w, b, gate, offs, pos1, pos2, out):
         biases = load_biases(EARLY_GELUS, E)
         nc.sync.dma_start(pos1_sb[:], pos1)
         nc.sync.dma_start(pos2_sb[:], pos2)
-        for t0 in (0, HALF):
-            nc.sync.dma_start(gates[:, :, t0 : t0 + HALF], gate[:, :, t0 : t0 + HALF].rearrange("r n t -> n r t"))
+        for which, t0, t1 in ((1, BOTH, T), (0, 0, PIECES[0][1]), (1, 0, BOTH), (0, PIECES[0][1], T)):
+            nc.sync.dma_start(gates[:, which, t0:t1], gate[which, :, t0:t1])
         for e in range(EARLY_GELUS, E - 1):
             activate(e, biases[e])
         multiply(E - 1)
         activate(E - 1, biases[E - 1])
 
-        def gated(name, pos_sb, which, t0, t1):
+        def fetch(name, pos_sb, t0, t1):
             tile = keep.tile([P, t1 - t0], F32, name=name, align_bytes=ALIGN)
-            idx = pos_sb[:, t0 // 16 : t1 // 16]
-            nc.vector.tensor_tensor(tile[:], y[:].indirect(idx), gates[:, which, t0:t1], MULT)
+            nc.scalar.activation(tile[:], y[:].indirect(pos_sb[:, t0 // 16 : t1 // 16]), COPY)
             return tile
 
-        added = keep.tile([P, ON_TENSOR], F32, name="added", align_bytes=ALIGN)
-        c1 = TENSOR_CUTS[1]
-        blocks = [slice(c, c + P) for c in range(0, c1, P)]
-        turned = [psum.tile([P, P], F32, name="sums") for block in blocks]
-        for which, pos_sb in enumerate((pos1_sb, pos2_sb)):
-            product = gated(f"turn{which}", pos_sb, which, 0, c1)
-            for bank, block in zip(turned, blocks):
-                nc.tensor.matmul(bank[:], product[:, block], identity[:], start=which == 0, stop=which == 1, is_transpose=True)
-        turned_sb = keep.tile([P, c1], F32, name="turned", align_bytes=ALIGN)
-        for bank, block in zip(turned, blocks):
-            nc.scalar.copy(turned_sb[:, block], bank[:])
-        bank = psum.tile([P, ON_TENSOR - c1], F32, name="sums")
-        nc.tensor.matmul(bank[:], identity[:], gated("first1", pos1_sb, 0, c1, ON_TENSOR)[:], start=True, stop=False)
-        back = psum.tile([P, c1], F32, name="sums")
-        for block in blocks:
-            nc.tensor.transpose(back[:, block], turned_sb[:, block], identity[:])
-        nc.scalar.copy(added[:, 0:c1], back[:])
-        nc.scalar.dma_start(out=out[:, 0:c1], in_=added[:, 0:c1])
-        nc.tensor.matmul(bank[:], identity[:], gated("second1", pos2_sb, 1, c1, ON_TENSOR)[:], start=False, stop=True)
-        nc.scalar.copy(added[:, c1:ON_TENSOR], bank[:])
-        nc.scalar.dma_start(out=out[:, c1:ON_TENSOR], in_=added[:, c1:ON_TENSOR])
-        first = gated("first", pos1_sb, 0, ON_TENSOR, T)
-        pieces = list(zip(VECTOR_CUTS, VECTOR_CUTS[1:]))
-        seconds = []
-        for i in range(len(pieces) + 1):
-            if i < len(pieces):
-                t0, t1 = pieces[i]
-                seconds.append(gated(f"second{t0}", pos2_sb, 1, t0, t1))
-            if i > 0:
-                t0, t1 = pieces[i - 1]
-                total = keep.tile([P, t1 - t0], F32, name=f"total{t0}", align_bytes=ALIGN)
-                nc.vector.tensor_tensor(total[:], first[:, t0 - ON_TENSOR : t1 - ON_TENSOR], seconds[i - 1][:], ADD)
-                nc.sync.dma_start(out=out[:, t0:t1], in_=total[:])
+        def weigh(tile, which, t0, t1):
+            nc.vector.tensor_tensor(tile[:], tile[:], gates[:, which, t0:t1], MULT)
+
+        def add_and_store(first, second, t0, t1):
+            nc.vector.tensor_tensor(first, first, second, ADD)
+            nc.sync.dma_start(out=out[:, t0:t1], in_=first)
+
+        seconds = keep.tile([P, T - BOTH], F32, name="seconds", align_bytes=ALIGN)
+        nc.vector.tensor_tensor(seconds[:], y[:].indirect(pos2_sb[:, BOTH // 16 :]), gates[:, 1, BOTH:], MULT)
+        (a0, a1), (b0, b1), (c0, c1) = PIECES
+        first_a = fetch("first_a", pos1_sb, a0, a1)
+        first = fetch("first", pos1_sb, 0, BOTH)
+        second = fetch("second", pos2_sb, 0, BOTH)
+        first_b = fetch("first_b", pos1_sb, b0, b1)
+        first_c = fetch("first_c", pos1_sb, c0, c1)
+        weigh(first_a, 0, a0, a1)
+        weigh(first, 0, 0, BOTH)
+        add_and_store(first_a[:], seconds[:, a0 - BOTH : a1 - BOTH], a0, a1)
+        weigh(second, 1, 0, BOTH)
+        weigh(first_b, 0, b0, b1)
+        add_and_store(first[:], second[:], 0, BOTH)
+        weigh(first_c, 0, c0, c1)
+        add_and_store(first_b[:], seconds[:, b0 - BOTH : b1 - BOTH], b0, b1)
+        add_and_store(first_c[:], seconds[:, c0 - BOTH : c1 - BOTH], c0, c1)

@@ -28,8 +28,8 @@ BIASES_BEHIND = 11
 EARLY_GELUS = 8
 BANKED = 8
 LAST_CUTS = ((0, 2), (2, 3), (3, 4))
-BOTH = 384
-PIECES = ((BOTH, 640), (640, 896), (896, T))
+BOTH = 320
+PIECES = ((BOTH, 768), (768, 896), (896, T))
 RAW_SLOT = PASSES * 4 * N * 4
 RAW_SLOTS = 10
 PAIRED = 8

@@ -32,7 +32,7 @@ BOTH = 320
 PIECES = ((BOTH, 768), (768, 896), (896, T))
 RAW_SLOT = PASSES * 4 * N * 4
 RAW_SLOTS = 10
-PAIRED = 8
+GROUPS = {0: 2, 2: 3, 5: 3, 8: 2}
 STAGE_BUFS = 9
 WEIGHT_BUFS = 5
 
@@ -137,8 +137,8 @@ def tile_routed_moe_kernel(tc, xT, w, b, gate, offs, pos1, pos2, out):
             nc.scalar.activation(y[:, e * C : (e + 1) * C], sums[e][:], GELU, bias=bias)
 
         for e in range(E - 2):
-            if e >= PAIRED or e % 2 == 0:
-                count = 2 if e < PAIRED else 1
+            if e >= 10 or e in GROUPS:
+                count = GROUPS.get(e, 1)
                 place = (2 * PASSES + e) % RAW_SLOTS * RAW_SLOT
                 loaded = raws.tile([P, count * PASSES, 4, N], F32, name=f"raw_w{e}", align_bytes=ALIGN, offset=place)
                 nc.sync.dma_start(out=loaded[:], in_=w_rows[:, e * PASSES : (e + count) * PASSES])

@@ -28,8 +28,9 @@ BIASES_BEHIND = 11
 EARLY_GELUS = 8
 BANKED = 8
 LAST_CUTS = ((0, 2), (2, 3), (3, 4))
-BOTH = 320
-PIECES = ((BOTH, 768), (768, 896), (896, T))
+BOTH = 256
+PIECES = ((BOTH, 704), (704, 896), (896, T))
+STORE = 160
 RAW_SLOT = PASSES * 4 * N * 4
 RAW_SLOTS = 10
 GROUPS = {0: 2, 2: 3, 5: 3, 8: 2}
@@ -185,7 +186,10 @@ def tile_routed_moe_kernel(tc, xT, w, b, gate, offs, pos1, pos2, out):
 
         def add_and_store(first, second, t0, t1):
             nc.vector.tensor_tensor(first, first, second, ADD)
-            nc.sync.dma_start(out=out[:, t0:t1], in_=first)
+            width = STORE if t1 - t0 > BOTH else t1 - t0
+            for c0 in range(0, t1 - t0, width):
+                c1 = min(c0 + width, t1 - t0)
+                nc.sync.dma_start(out=out[:, t0 + c0 : t0 + c1], in_=first[:, c0:c1])
 
         seconds = keep.tile([P, T - BOTH], F32, name="seconds", align_bytes=ALIGN)
         nc.vector.tensor_tensor(seconds[:], y[:].indirect(pos2_sb[:, BOTH // 16 :]), gates[:, 1, BOTH:], MULT)

@@ -26,6 +26,7 @@ WHOLE_ON_VECTOR = (7, 9)
 SHARED_FROM = 11
 BIASES_BEHIND = 11
 EARLY_GELUS = 8
+ON_GPSIMD = 5
 BANKED = 8
 LAST_CUTS = ((0, 2), (2, 3), (3, 4))
 BOTH = 256
@@ -33,7 +34,7 @@ PIECES = ((BOTH, 704), (704, 896), (896, T))
 STORE = 160
 RAW_SLOT = PASSES * 4 * N * 4
 RAW_SLOTS = 10
-GROUPS = {0: 2, 2: 3, 5: 3, 8: 2}
+GROUPS = {0: 3, 3: 3, 6: 2, 8: 2}
 STAGE_BUFS = 9
 WEIGHT_BUFS = 5
 
@@ -71,6 +72,10 @@ def tile_routed_moe_kernel(tc, xT, w, b, gate, offs, pos1, pos2, out):
             grouped = stage.tile([P, passes, columns, 4], BF16, name="grouped", align_bytes=ALIGN)
             src = raw.rearrange("p a j (c i) -> p a c j i", i=4)
             dst = grouped[:].rearrange("p a (c i) j -> p a c j i", i=4)
+            if share is None:
+                for a in range(passes):
+                    nc.gpsimd.tensor_scalar(dst[:, a], src[:, a], 1.0, 0.0, MULT, ADD)
+                return grouped[:].rearrange("p a c j -> p (a c j)")
             cut = int(share * columns) // 4
             if cut > 0:
                 nc.vector.tensor_copy(dst[:, :, 0:cut], src[:, :, 0:cut])
@@ -80,7 +85,7 @@ def tile_routed_moe_kernel(tc, xT, w, b, gate, offs, pos1, pos2, out):
 
         x_rows = xT.rearrange("(a p j) t -> p a j t", p=P, j=4)
         for a in range(PASSES):
-            raw = raws.tile([P, 1, 4, T], F32, name=f"raw_x{a}", align_bytes=ALIGN, offset=2 * a * RAW_SLOT)
+            raw = raws.tile([P, 1, 4, T], F32, name=f"raw_x{a}", align_bytes=ALIGN, offset=(2 + 2 * a) * RAW_SLOT)
             nc.sync.dma_start(out=raw[:], in_=x_rows[:, a : a + 1])
             width = QUARTER if a == 0 else HALF
             for t0 in range(0, T, width):
@@ -140,7 +145,7 @@ def tile_routed_moe_kernel(tc, xT, w, b, gate, offs, pos1, pos2, out):
         for e in range(E - 2):
             if e >= 10 or e in GROUPS:
                 count = GROUPS.get(e, 1)
-                place = (2 * PASSES + e) % RAW_SLOTS * RAW_SLOT
+                place = e % RAW_SLOTS * RAW_SLOT
                 loaded = raws.tile([P, count * PASSES, 4, N], F32, name=f"raw_w{e}", align_bytes=ALIGN, offset=place)
                 nc.sync.dma_start(out=loaded[:], in_=w_rows[:, e * PASSES : (e + count) * PASSES])
                 first_loaded = e
@@ -150,13 +155,13 @@ def tile_routed_moe_kernel(tc, xT, w, b, gate, offs, pos1, pos2, out):
             if e >= SHARED_FROM or e in WHOLE_ON_VECTOR:
                 quantise_weights(e, [(0, raw[:, 0:2], True), (2, raw[:, 2:4], e < SHARED_FROM)])
             else:
-                quantise_weights(e, [(0, raw, False)])
+                quantise_weights(e, [(0, raw, None if e == ON_GPSIMD else False)])
             if e == BIASES_BEHIND:
                 for done in range(EARLY_GELUS):
                     activate(done, biases[done])
             multiply(e)
         for a0 in (0, 2):
-            place = (2 * PASSES + E - 2) % RAW_SLOTS * RAW_SLOT + a0 * (RAW_SLOT // PASSES)
+            place = (E - 2) % RAW_SLOTS * RAW_SLOT + a0 * (RAW_SLOT // PASSES)
             raw = raws.tile([P, 2, 4, N], F32, name=f"raw_before_last{a0}", align_bytes=ALIGN, offset=place)
             nc.sync.dma_start(out=raw[:], in_=w_rows[:, (E - 2) * PASSES + a0 : (E - 2) * PASSES + a0 + 2])
             quantise_weights(E - 2, [(a0, raw[:, 0:1], 1), (a0 + 1, raw[:, 1:2], 0)])

@@ -28,6 +28,7 @@ BIASES_BEHIND = 11
 EARLY_GELUS = 8
 ON_GPSIMD = 5
 BANKED = 8
+HELD = (13, 11, 12)
 LAST_CUTS = ((0, 2), (2, 3), (3, 4))
 BOTH = 256
 PIECES = ((BOTH, 704), (704, 896), (896, T))
@@ -36,7 +37,7 @@ RAW_SLOT = PASSES * 4 * N * 4
 RAW_SLOTS = 10
 GROUPS = {0: 3, 3: 3, 6: 2, 8: 2}
 STAGE_BUFS = 9
-WEIGHT_BUFS = 5
+WEIGHT_BUFS = 6
 
 
 def tile_routed_moe_kernel(tc, xT, w, b, gate, offs, pos1, pos2, out):
@@ -115,9 +116,13 @@ def tile_routed_moe_kernel(tc, xT, w, b, gate, offs, pos1, pos2, out):
 
         def multiply(e):
             w_words, w_scales = weights[e]
-            if e >= BANKED:
+            if e == HELD[0]:
+                bank = psum.tile([P, len(HELD), C], F32, name="sums")
+                for i, held in enumerate(HELD):
+                    sums[held] = bank[:, i]
+            elif e >= BANKED and e not in HELD:
                 sums[e] = psum.tile([P, C], F32, name="sums")
-            elif e % 4 == 0:
+            elif e < BANKED and e % 4 == 0:
                 bank = psum.tile([P, 4, C], F32, name="sums")
                 for i in range(4):
                     sums[e + i] = bank[:, i]
@@ -159,6 +164,9 @@ def tile_routed_moe_kernel(tc, xT, w, b, gate, offs, pos1, pos2, out):
             if e == BIASES_BEHIND:
                 for done in range(EARLY_GELUS):
                     activate(done, biases[done])
+            if e not in HELD:
+                multiply(e)
+        for e in HELD:
             multiply(e)
         for a0 in (0, 2):
             place = (E - 2) % RAW_SLOTS * RAW_SLOT + a0 * (RAW_SLOT // PASSES)

@@ -22,20 +22,23 @@ HALF, QUARTER = T // 2, T // 4
 ALIGN = 256
 
 WINDOW = 2 * SLOTS
-WHOLE_ON_VECTOR = (7, 9)
+RAW_SLOT = PASSES * 4 * N * 4
+RAW_SLOTS = 10
+X_SLOT = 2
+GROUPS = {0: 3, 3: 3, 6: 2, 8: 2}
+SINGLE_FROM = 10
+ON_GPSIMD = 5
+WHOLE_ON_VECTOR = (9,)
 SHARED_FROM = 11
+LAST_COPIERS = ("vector", "scalar", "scalar", "vector")
 BIASES_BEHIND = 11
 EARLY_GELUS = 8
-ON_GPSIMD = 5
 BANKED = 8
 HELD = (13, 11, 12)
 LAST_CUTS = ((0, 2), (2, 3), (3, 4))
 BOTH = 256
-PIECES = ((BOTH, 704), (704, 896), (896, T))
+LARGE, MIDDLE, SMALL = slice(BOTH, 704), slice(704, 896), slice(896, T)
 STORE = 160
-RAW_SLOT = PASSES * 4 * N * 4
-RAW_SLOTS = 10
-GROUPS = {0: 3, 3: 3, 6: 2, 8: 2}
 STAGE_BUFS = 9
 WEIGHT_BUFS = 6
 
@@ -68,29 +71,28 @@ def tile_routed_moe_kernel(tc, xT, w, b, gate, offs, pos1, pos2, out):
             x_words.append(all_words[:, start : start + WINDOW])
             slot_words.append(keep.tile([P, SLOTS], U32, name=f"slot_words{a}", align_bytes=ALIGN))
 
-        def interleave(raw, share):
+        def interleave(raw, copier):
             passes, columns = raw.shape[1], raw.shape[3]
             grouped = stage.tile([P, passes, columns, 4], BF16, name="grouped", align_bytes=ALIGN)
             src = raw.rearrange("p a j (c i) -> p a c j i", i=4)
             dst = grouped[:].rearrange("p a (c i) j -> p a c j i", i=4)
-            if share is None:
+            if copier == "vector":
+                nc.vector.tensor_copy(dst, src)
+            elif copier == "scalar":
+                nc.scalar.copy(dst, src)
+            else:
                 for a in range(passes):
                     nc.gpsimd.tensor_scalar(dst[:, a], src[:, a], 1.0, 0.0, MULT, ADD)
-                return grouped[:].rearrange("p a c j -> p (a c j)")
-            cut = int(share * columns) // 4
-            if cut > 0:
-                nc.vector.tensor_copy(dst[:, :, 0:cut], src[:, :, 0:cut])
-            if cut < columns // 4:
-                nc.scalar.copy(dst[:, :, cut:], src[:, :, cut:])
             return grouped[:].rearrange("p a c j -> p (a c j)")
 
         x_rows = xT.rearrange("(a p j) t -> p a j t", p=P, j=4)
         for a in range(PASSES):
-            raw = raws.tile([P, 1, 4, T], F32, name=f"raw_x{a}", align_bytes=ALIGN, offset=(2 + 2 * a) * RAW_SLOT)
+            place = (X_SLOT + 2 * a) * RAW_SLOT
+            raw = raws.tile([P, 1, 4, T], F32, name=f"raw_x{a}", align_bytes=ALIGN, offset=place)
             nc.sync.dma_start(out=raw[:], in_=x_rows[:, a : a + 1])
             width = QUARTER if a == 0 else HALF
             for t0 in range(0, T, width):
-                grouped = interleave(raw[:, :, :, t0 : t0 + width], a == 0 and t0 < HALF)
+                grouped = interleave(raw[:, :, :, t0 : t0 + width], "vector" if a == 0 and t0 < HALF else "scalar")
                 cols = slice(t0, t0 + width)
                 nc.vector.quantize_mx(
                     out=x_words[a][:, cols].bitcast(FP8X4), scales=x_scales[4 * a : P, cols], in_=grouped
@@ -109,7 +111,7 @@ def tile_routed_moe_kernel(tc, xT, w, b, gate, offs, pos1, pos2, out):
                 w_scales = wts.tile([P, PASSES * N], U8, name="w_scales", align_bytes=ALIGN)
                 weights[e] = (w_words, w_scales)
             w_words, w_scales = weights[e]
-            copied = [(a0, raw.shape[1], interleave(raw, share)) for a0, raw, share in parts]
+            copied = [(a0, raw.shape[1], interleave(raw, copier)) for a0, raw, copier in parts]
             for a0, passes, grouped in copied:
                 cols = slice(a0 * N, (a0 + passes) * N)
                 nc.vector.quantize_mx(out=w_words[:, cols].bitcast(FP8X4), scales=w_scales[:, cols], in_=grouped)
@@ -148,7 +150,7 @@ def tile_routed_moe_kernel(tc, xT, w, b, gate, offs, pos1, pos2, out):
             nc.scalar.activation(y[:, e * C : (e + 1) * C], sums[e][:], GELU, bias=bias)
 
         for e in range(E - 2):
-            if e >= 10 or e in GROUPS:
+            if e >= SINGLE_FROM or e in GROUPS:
                 count = GROUPS.get(e, 1)
                 place = e % RAW_SLOTS * RAW_SLOT
                 loaded = raws.tile([P, count * PASSES, 4, N], F32, name=f"raw_w{e}", align_bytes=ALIGN, offset=place)
@@ -158,9 +160,10 @@ def tile_routed_moe_kernel(tc, xT, w, b, gate, offs, pos1, pos2, out):
             if e == BIASES_BEHIND:
                 biases = load_biases(0, EARLY_GELUS)
             if e >= SHARED_FROM or e in WHOLE_ON_VECTOR:
-                quantise_weights(e, [(0, raw[:, 0:2], True), (2, raw[:, 2:4], e < SHARED_FROM)])
+                later = "vector" if e in WHOLE_ON_VECTOR else "scalar"
+                quantise_weights(e, [(0, raw[:, 0:2], "vector"), (2, raw[:, 2:4], later)])
             else:
-                quantise_weights(e, [(0, raw, None if e == ON_GPSIMD else False)])
+                quantise_weights(e, [(0, raw, "gpsimd" if e == ON_GPSIMD else "scalar")])
             if e == BIASES_BEHIND:
                 for done in range(EARLY_GELUS):
                     activate(done, biases[done])
@@ -172,52 +175,54 @@ def tile_routed_moe_kernel(tc, xT, w, b, gate, offs, pos1, pos2, out):
             place = (E - 2) % RAW_SLOTS * RAW_SLOT + a0 * (RAW_SLOT // PASSES)
             raw = raws.tile([P, 2, 4, N], F32, name=f"raw_before_last{a0}", align_bytes=ALIGN, offset=place)
             nc.sync.dma_start(out=raw[:], in_=w_rows[:, (E - 2) * PASSES + a0 : (E - 2) * PASSES + a0 + 2])
-            quantise_weights(E - 2, [(a0, raw[:, 0:1], 1), (a0 + 1, raw[:, 1:2], 0)])
+            quantise_weights(E - 2, [(a0, raw[:, 0:1], "vector"), (a0 + 1, raw[:, 1:2], "scalar")])
         multiply(E - 2)
         for a0, a1 in LAST_CUTS:
             raw = keep.tile([P, a1 - a0, 4, N], F32, name=f"raw_last{a0}", align_bytes=ALIGN)
             nc.sync.dma_start(out=raw[:], in_=w_rows[:, (E - 1) * PASSES + a0 : (E - 1) * PASSES + a1])
-            quantise_weights(E - 1, [(a, raw[:, a - a0 : a - a0 + 1], (1, 0, 0, 1)[a]) for a in range(a0, a1)])
+            quantise_weights(E - 1, [(a, raw[:, a - a0 : a - a0 + 1], LAST_COPIERS[a]) for a in range(a0, a1)])
 
         biases = load_biases(EARLY_GELUS, E)
         nc.sync.dma_start(pos1_sb[:], pos1)
         nc.sync.dma_start(pos2_sb[:], pos2)
-        for which, t0, t1 in ((1, BOTH, T), (0, 0, PIECES[0][1]), (1, 0, BOTH), (0, PIECES[0][1], T)):
+        for which, t0, t1 in ((1, BOTH, T), (0, 0, LARGE.stop), (1, 0, BOTH), (0, LARGE.stop, T)):
             nc.sync.dma_start(gates[:, which, t0:t1], gate[which, :, t0:t1])
         for e in range(EARLY_GELUS, E - 1):
             activate(e, biases[e])
         multiply(E - 1)
         activate(E - 1, biases[E - 1])
 
-        def fetch(name, pos_sb, t0, t1):
-            tile = keep.tile([P, t1 - t0], F32, name=name, align_bytes=ALIGN)
-            nc.scalar.activation(tile[:], y[:].indirect(pos_sb[:, t0 // 16 : t1 // 16]), COPY)
-            return tile
+        def fetch(name, pos_sb, tokens):
+            tile = keep.tile([P, tokens.stop - tokens.start], F32, name=name, align_bytes=ALIGN)
+            nc.scalar.activation(tile[:], y[:].indirect(pos_sb[:, tokens.start // 16 : tokens.stop // 16]), COPY)
+            return tile[:]
 
-        def weigh(tile, which, t0, t1):
-            nc.vector.tensor_tensor(tile[:], tile[:], gates[:, which, t0:t1], MULT)
+        def weigh(fetched, which, tokens):
+            nc.vector.tensor_tensor(fetched, fetched, gates[:, which, tokens], MULT)
 
-        def add_and_store(first, second, t0, t1):
+        def add_and_store(first, second, tokens, width):
             nc.vector.tensor_tensor(first, first, second, ADD)
-            width = STORE if t1 - t0 > BOTH else t1 - t0
-            for c0 in range(0, t1 - t0, width):
-                c1 = min(c0 + width, t1 - t0)
-                nc.sync.dma_start(out=out[:, t0 + c0 : t0 + c1], in_=first[:, c0:c1])
+            for t0 in range(tokens.start, tokens.stop, width):
+                t1 = min(t0 + width, tokens.stop)
+                nc.sync.dma_start(out=out[:, t0:t1], in_=first[:, t0 - tokens.start : t1 - tokens.start])
 
+        low = slice(0, BOTH)
         seconds = keep.tile([P, T - BOTH], F32, name="seconds", align_bytes=ALIGN)
         nc.vector.tensor_tensor(seconds[:], y[:].indirect(pos2_sb[:, BOTH // 16 :]), gates[:, 1, BOTH:], MULT)
-        (a0, a1), (b0, b1), (c0, c1) = PIECES
-        first_a = fetch("first_a", pos1_sb, a0, a1)
-        first = fetch("first", pos1_sb, 0, BOTH)
-        second = fetch("second", pos2_sb, 0, BOTH)
-        first_b = fetch("first_b", pos1_sb, b0, b1)
-        first_c = fetch("first_c", pos1_sb, c0, c1)
-        weigh(first_a, 0, a0, a1)
-        weigh(first, 0, 0, BOTH)
-        add_and_store(first_a[:], seconds[:, a0 - BOTH : a1 - BOTH], a0, a1)
-        weigh(second, 1, 0, BOTH)
-        weigh(first_b, 0, b0, b1)
-        add_and_store(first[:], second[:], 0, BOTH)
-        weigh(first_c, 0, c0, c1)
-        add_and_store(first_b[:], seconds[:, b0 - BOTH : b1 - BOTH], b0, b1)
-        add_and_store(first_c[:], seconds[:, c0 - BOTH : c1 - BOTH], c0, c1)
+        second_large, second_middle, second_small = (
+            seconds[:, tokens.start - BOTH : tokens.stop - BOTH] for tokens in (LARGE, MIDDLE, SMALL)
+        )
+        first_large = fetch("first_large", pos1_sb, LARGE)
+        first_low = fetch("first_low", pos1_sb, low)
+        second_low = fetch("second_low", pos2_sb, low)
+        first_middle = fetch("first_middle", pos1_sb, MIDDLE)
+        first_small = fetch("first_small", pos1_sb, SMALL)
+        weigh(first_large, 0, LARGE)
+        weigh(first_low, 0, low)
+        add_and_store(first_large, second_large, LARGE, STORE)
+        weigh(second_low, 1, low)
+        weigh(first_middle, 0, MIDDLE)
+        add_and_store(first_low, second_low, low, T)
+        weigh(first_small, 0, SMALL)
+        add_and_store(first_middle, second_middle, MIDDLE, T)
+        add_and_store(first_small, second_small, SMALL, T)

from contextlib import ExitStack

import concourse.mybir as mybir

K, T, E, C, N = 2048, 1024, 16, 128, 128
FLOPS = 2 * K * E * C * N

F32 = mybir.dt.float32
BF16 = mybir.dt.bfloat16
U32 = mybir.dt.uint32
U16 = mybir.dt.uint16
U8 = mybir.dt.uint8
FP8X4 = mybir.dt.float8_e4m3fn_x4
MULT, ADD = mybir.AluOpType.mult, mybir.AluOpType.add
GELU = mybir.ActivationFunctionType.Gelu_apprx_tanh
COPY = mybir.ActivationFunctionType.Copy

P = 128
PASSES = K // 512
SLOTS = E * C
HALF, QUARTER = T // 2, T // 4
ALIGN = 256

WINDOW = 2 * SLOTS
RAW_SLOT = PASSES * 4 * N * 4
RAW_SLOTS = 10
X_SLOT = 2
GROUPS = {0: 3, 3: 3, 6: 2, 8: 2}
SINGLE_FROM = 10
ON_GPSIMD = 5
WHOLE_ON_VECTOR = (9,)
SHARED_FROM = 11
LAST_COPIERS = ("vector", "scalar", "scalar", "vector")
BIASES_BEHIND = 11
EARLY_GELUS = 8
BANKED = 8
HELD = (13, 11, 12)
LAST_CUTS = ((0, 2), (2, 3), (3, 4))
BOTH = 256
LARGE, MIDDLE, SMALL = slice(BOTH, 704), slice(704, 896), slice(896, T)
STORE = 160
STAGE_BUFS = 9
WEIGHT_BUFS = 6


def tile_routed_moe_kernel(tc, xT, w, b, gate, offs, pos1, pos2, out):
    nc = tc.nc
    with ExitStack() as ctx:
        keep = ctx.enter_context(tc.tile_pool(name="keep", bufs=1))
        raws = ctx.enter_context(tc.tile_pool(name="raws", bufs=1))
        stage = ctx.enter_context(tc.tile_pool(name="stage", bufs=STAGE_BUFS))
        wts = ctx.enter_context(tc.tile_pool(name="wts", bufs=WEIGHT_BUFS))
        psum = ctx.enter_context(tc.psum_pool(name="psum", bufs=8))

        warm = keep.tile([P, 2], F32, name="warm")
        nc.gpsimd.memset(warm[:], 0.0)
        nc.scalar.activation(warm[:, 1:2], warm[:, 0:1], GELU)
        x_scales = keep.tile([P, WINDOW], U8, name="x_scales", align_bytes=ALIGN)
        nc.gpsimd.memset(x_scales[:, 0:T], 0)

        offs_sb = keep.tile([P, SLOTS // 16], U16, name="offs_sb")
        pos1_sb = keep.tile([P, T // 16], U16, name="pos1_sb")
        pos2_sb = keep.tile([P, T // 16], U16, name="pos2_sb")
        y = keep.tile([P, SLOTS], F32, name="y", align_bytes=ALIGN)
        gates = keep.tile([P, 2, T], F32, name="gates", align_bytes=ALIGN)
        slot_scales = keep.tile([P, SLOTS], U8, name="slot_scales", align_bytes=ALIGN)
        all_words = keep.tile([P, (PASSES - 1) * T + WINDOW], U32, name="all_words", align_bytes=ALIGN)
        x_words, slot_words = [], []
        for a in range(PASSES):
            start = (PASSES - 1 - a) * T
            x_words.append(all_words[:, start : start + WINDOW])
            slot_words.append(keep.tile([P, SLOTS], U32, name=f"slot_words{a}", align_bytes=ALIGN))

        def interleave(raw, copier):
            passes, columns = raw.shape[1], raw.shape[3]
            grouped = stage.tile([P, passes, columns, 4], BF16, name="grouped", align_bytes=ALIGN)
            src = raw.rearrange("p a j (c i) -> p a c j i", i=4)
            dst = grouped[:].rearrange("p a (c i) j -> p a c j i", i=4)
            if copier == "vector":
                nc.vector.tensor_copy(dst, src)
            elif copier == "scalar":
                nc.scalar.copy(dst, src)
            else:
                for a in range(passes):
                    nc.gpsimd.tensor_scalar(dst[:, a], src[:, a], 1.0, 0.0, MULT, ADD)
            return grouped[:].rearrange("p a c j -> p (a c j)")

        x_rows = xT.rearrange("(a p j) t -> p a j t", p=P, j=4)
        for a in range(PASSES):
            place = (X_SLOT + 2 * a) * RAW_SLOT
            raw = raws.tile([P, 1, 4, T], F32, name=f"raw_x{a}", align_bytes=ALIGN, offset=place)
            nc.sync.dma_start(out=raw[:], in_=x_rows[:, a : a + 1])
            width = QUARTER if a == 0 else HALF
            for t0 in range(0, T, width):
                grouped = interleave(raw[:, :, :, t0 : t0 + width], "vector" if a == 0 and t0 < HALF else "scalar")
                cols = slice(t0, t0 + width)
                nc.vector.quantize_mx(
                    out=x_words[a][:, cols].bitcast(FP8X4), scales=x_scales[4 * a : P, cols], in_=grouped
                )
            if a == 0:
                nc.sync.dma_start(offs_sb[:], offs)
            nc.vector.tensor_copy(slot_words[a][:], x_words[a].indirect(offs_sb[:]))
        nc.vector.tensor_copy(slot_scales[:], x_scales[:].indirect(offs_sb[:]))

        w_rows = w.rearrange("e (a p j) n -> p (e a) j n", p=P, j=4)
        weights, sums = {}, {}

        def quantise_weights(e, parts):
            if e not in weights:
                w_words = wts.tile([P, PASSES * N], U32, name="w_words", align_bytes=ALIGN)
                w_scales = wts.tile([P, PASSES * N], U8, name="w_scales", align_bytes=ALIGN)
                weights[e] = (w_words, w_scales)
            w_words, w_scales = weights[e]
            copied = [(a0, raw.shape[1], interleave(raw, copier)) for a0, raw, copier in parts]
            for a0, passes, grouped in copied:
                cols = slice(a0 * N, (a0 + passes) * N)
                nc.vector.quantize_mx(out=w_words[:, cols].bitcast(FP8X4), scales=w_scales[:, cols], in_=grouped)

        def multiply(e):
            w_words, w_scales = weights[e]
            if e == HELD[0]:
                bank = psum.tile([P, len(HELD), C], F32, name="sums")
                for i, held in enumerate(HELD):
                    sums[held] = bank[:, i]
            elif e >= BANKED and e not in HELD:
                sums[e] = psum.tile([P, C], F32, name="sums")
            elif e < BANKED and e % 4 == 0:
                bank = psum.tile([P, 4, C], F32, name="sums")
                for i in range(4):
                    sums[e + i] = bank[:, i]
            slots = slice(e * C, (e + 1) * C)
            for a in range(PASSES):
                cols = slice(a * N, (a + 1) * N)
                nc.tensor.matmul_mx(
                    out=sums[e][:],
                    lhsT=w_words[:, cols].bitcast(FP8X4),
                    lhsT_scale=w_scales[:, cols],
                    rhs=slot_words[a][:, slots].bitcast(FP8X4),
                    rhs_scale=slot_scales[4 * a : P, slots],
                    start=(a == 0),
                    stop=(a == PASSES - 1),
                )

        def load_biases(e0, e1):
            tile = keep.tile([P, e1 - e0], F32, name=f"biases{e0}")
            nc.sync.dma_start(tile[:], b[:, e0:e1])
            return {e: tile[:, e - e0 : e - e0 + 1] for e in range(e0, e1)}

        def activate(e, bias):
            nc.scalar.activation(y[:, e * C : (e + 1) * C], sums[e][:], GELU, bias=bias)

        for e in range(E - 2):
            if e >= SINGLE_FROM or e in GROUPS:
                count = GROUPS.get(e, 1)
                place = e % RAW_SLOTS * RAW_SLOT
                loaded = raws.tile([P, count * PASSES, 4, N], F32, name=f"raw_w{e}", align_bytes=ALIGN, offset=place)
                nc.sync.dma_start(out=loaded[:], in_=w_rows[:, e * PASSES : (e + count) * PASSES])
                first_loaded = e
            raw = loaded[:, (e - first_loaded) * PASSES : (e - first_loaded + 1) * PASSES]
            if e == BIASES_BEHIND:
                biases = load_biases(0, EARLY_GELUS)
            if e >= SHARED_FROM or e in WHOLE_ON_VECTOR:
                later = "vector" if e in WHOLE_ON_VECTOR else "scalar"
                quantise_weights(e, [(0, raw[:, 0:2], "vector"), (2, raw[:, 2:4], later)])
            else:
                quantise_weights(e, [(0, raw, "gpsimd" if e == ON_GPSIMD else "scalar")])
            if e == BIASES_BEHIND:
                for done in range(EARLY_GELUS):
                    activate(done, biases[done])
            if e not in HELD:
                multiply(e)
        for e in HELD:
            multiply(e)
        for a0 in (0, 2):
            place = (E - 2) % RAW_SLOTS * RAW_SLOT + a0 * (RAW_SLOT // PASSES)
            raw = raws.tile([P, 2, 4, N], F32, name=f"raw_before_last{a0}", align_bytes=ALIGN, offset=place)
            nc.sync.dma_start(out=raw[:], in_=w_rows[:, (E - 2) * PASSES + a0 : (E - 2) * PASSES + a0 + 2])
            quantise_weights(E - 2, [(a0, raw[:, 0:1], "vector"), (a0 + 1, raw[:, 1:2], "scalar")])
        multiply(E - 2)
        for a0, a1 in LAST_CUTS:
            raw = keep.tile([P, a1 - a0, 4, N], F32, name=f"raw_last{a0}", align_bytes=ALIGN)
            nc.sync.dma_start(out=raw[:], in_=w_rows[:, (E - 1) * PASSES + a0 : (E - 1) * PASSES + a1])
            quantise_weights(E - 1, [(a, raw[:, a - a0 : a - a0 + 1], LAST_COPIERS[a]) for a in range(a0, a1)])

        biases = load_biases(EARLY_GELUS, E)
        nc.sync.dma_start(pos1_sb[:], pos1)
        nc.sync.dma_start(pos2_sb[:], pos2)
        for which, t0, t1 in ((1, BOTH, T), (0, 0, LARGE.stop), (1, 0, BOTH), (0, LARGE.stop, T)):
            nc.sync.dma_start(gates[:, which, t0:t1], gate[which, :, t0:t1])
        for e in range(EARLY_GELUS, E - 1):
            activate(e, biases[e])
        multiply(E - 1)
        activate(E - 1, biases[E - 1])

        def fetch(name, pos_sb, tokens):
            tile = keep.tile([P, tokens.stop - tokens.start], F32, name=name, align_bytes=ALIGN)
            nc.scalar.activation(tile[:], y[:].indirect(pos_sb[:, tokens.start // 16 : tokens.stop // 16]), COPY)
            return tile[:]

        def weigh(fetched, which, tokens):
            nc.vector.tensor_tensor(fetched, fetched, gates[:, which, tokens], MULT)

        def add_and_store(first, second, tokens, width):
            nc.vector.tensor_tensor(first, first, second, ADD)
            for t0 in range(tokens.start, tokens.stop, width):
                t1 = min(t0 + width, tokens.stop)
                nc.sync.dma_start(out=out[:, t0:t1], in_=first[:, t0 - tokens.start : t1 - tokens.start])

        low = slice(0, BOTH)
        seconds = keep.tile([P, T - BOTH], F32, name="seconds", align_bytes=ALIGN)
        nc.vector.tensor_tensor(seconds[:], y[:].indirect(pos2_sb[:, BOTH // 16 :]), gates[:, 1, BOTH:], MULT)
        second_large, second_middle, second_small = (
            seconds[:, tokens.start - BOTH : tokens.stop - BOTH] for tokens in (LARGE, MIDDLE, SMALL)
        )
        first_large = fetch("first_large", pos1_sb, LARGE)
        first_low = fetch("first_low", pos1_sb, low)
        second_low = fetch("second_low", pos2_sb, low)
        first_middle = fetch("first_middle", pos1_sb, MIDDLE)
        first_small = fetch("first_small", pos1_sb, SMALL)
        weigh(first_large, 0, LARGE)
        weigh(first_low, 0, low)
        add_and_store(first_large, second_large, LARGE, STORE)
        weigh(second_low, 1, low)
        weigh(first_middle, 0, MIDDLE)
        add_and_store(first_low, second_low, low, T)
        weigh(first_small, 0, SMALL)
        add_and_store(first_middle, second_middle, MIDDLE, T)
        add_and_store(first_small, second_small, SMALL, T)
